import numpy as np, ml_dtypes
CORES = [10,34,74,98]
N = 4
BF = ml_dtypes.bfloat16
def gentries(a):
    return np.ascontiguousarray(a.reshape(8, 16, -1).transpose(0, 2, 1)).reshape(8, -1)
def gtable(e):
    e = np.asarray(e); return np.ascontiguousarray(e.reshape(8, -1, 16).transpose(0, 2, 1)).reshape(128, -1).astype(np.int32)
T, P, R, CAP = 512, 4096, 4, 256
def put(o):
    return np.stack([gtable(o[r].reshape(8, -1).astype(np.int32)) for r in range(N)])
def get(came):
    return np.stack([gentries(came[r]).reshape(8, R, N - 1, T) for r in range(N)])
def start(rng):
    o = np.stack([rng.permutation(8) for r in range(N)])
    s = np.array([16, 16, 16, 12, 12, 8, 4, 2])[o]; c = np.array([1, 1, 2, 2, 0, 2, 1, 0])[o]
    had = np.array([P // 2, 3 * P // 4, P])[c] + rng.integers(0, np.array([P // 8, P // 4, P + 1])[c])
    n = (rng.integers(0, CAP + 1, (N, 8, R, N - 1)) * s[:, :, None, None]) >> 4
    for r in range(N):
        n[r, rng.integers(0, 8), rng.integers(0, R), rng.integers(0, N - 1)] = 0
        n[r, np.argmax(s[r]), rng.integers(0, R), rng.integers(0, N - 1)] = CAP
    return had[:, :, None].astype(np.int32), n
def consts(rng):
    h = np.zeros((N, 8, 6 * R + 3), np.int32)
    for e in range(R):
        h[:, :, 6 * e:6 * e + 3] = 2 * rng.integers(0, 2048, (N, 8, 3)) + 1
        h[:, :, 6 * e + 3:6 * e + 6] = rng.integers(0, 4096, (N, 8, 3))
    h[:, :, 6 * R:] = 2 * rng.integers(0, 128, (N, 8, 3)) + 1
    return h
def arrivals(rng, n):
    o = np.argsort(np.argsort(rng.random((N, 8, R, N - 1, T)), -1), -1)
    return put(o < n[..., None])
def setup_inputs(rng):
    had, n = start(rng)
    return {"ring": rng.integers(0, 256, (N, 128, P)).astype(np.float32).astype(BF), "had": had, "hc": consts(rng), "came": arrivals(rng, n)}
def setup_inputs_full(rng):
    d = setup_inputs(rng); d["came"] = arrivals(rng, np.full((N, 8, R, N - 1), CAP))
    v = np.array([P // 2, P - 1, P, 2 * P, P + 1, 2 * P - 1, P // 2 + 1, 3 * P // 2])
    d["had"] = np.stack([rng.permutation(v) for r in range(N)])[:, :, None].astype(np.int32); return d
def setup_inputs_lost(rng):
    d = setup_inputs(rng); o = get(d["came"]) > 0; z = rng.integers(0, N)
    for r in range(N):
        w = rng.permutation(8)
        o[r, w[0]] = False
        o[r, w[1]] = False; o[r, w[1], :, :, 0] = True
        o[r, w[2]] = False; o[r, w[2], :, :, T - 1] = True
        o[r, w[3], rng.integers(0, R)] = False
        o[r, w[4], :, :N - 2] = False
    o[z] = False
    d["came"] = put(o); return d
def setup_inputs_ends(rng):
    d = setup_inputs(rng); o = get(d["came"]); hc = d["hc"]
    n0 = np.sum(o[:, :, 0], axis=(2, 3)); v = np.array([P, P - 1, P + 1, 2 * P, 2 * P - 1, P, 2 * P, P + 1])
    d["had"] = (np.stack([rng.permutation(v) for r in range(N)]) - n0)[:, :, None].astype(np.int32)
    a = np.arange(4096); top = int(np.flatnonzero(((2 * ((a * a) & 2047) + a) & 4095) == 4095)[0])
    for q in range(N):
        for e in range(R):
            for g in range(8):
                dd = int(rng.integers(1, N)); r = (q - dd) % N; w = np.flatnonzero(o[r, g, e, dd - 1])
                x = r * T + (int(rng.choice(w)) if w.size else 0)
                for k, u in ((0, 0), (1, top)): hc[q, g, 6 * e + 3 + k] = (u - int(hc[q, g, 6 * e + k]) * x) & 4095
                if g & 1:
                    hc[q, g, 6 * e + 2] = hc[q, g, 6 * e]; hc[q, g, 6 * e + 5] = hc[q, g, 6 * e + 3]
    return d
def setup_inputs_bursts(rng):
    d = setup_inputs(rng); had, n = start(rng); d["had"] = had
    a = rng.integers(0, T - n + 1); b = np.where(rng.random(n.shape) < 0.5, 0, T - n)
    a[:, ::2] = b[:, ::2]; t = np.arange(T)
    d["came"] = put((t >= a[..., None]) & (t < (a + n)[..., None])); return d
def setup_inputs_spread(rng):
    d = setup_inputs(rng)
    d["ring"] = (rng.integers(0, 256, (N, 128, P)) >> rng.integers(0, 9, (N, 1, P))).astype(np.float32).astype(BF)
    d["had"] = rng.integers(P // 2, 2 * P + 1, (N, 8, 1)).astype(np.int32)
    hc = d["hc"]; m = rng.random(hc.shape) < 0.25; lo = np.zeros(6 * R + 3, np.int64); hi = np.full(6 * R + 3, 4095)
    for e in range(R): lo[6 * e:6 * e + 3] = 1
    lo[6 * R:] = 1; hi[6 * R:] = 255
    d["hc"] = np.where(m, np.where(rng.random(hc.shape) < 0.5, lo, hi), hc).astype(np.int32)
    n = np.floor(rng.random((N, 8, R, N - 1)) ** 3 * (CAP + 1)).astype(np.int64)
    d["came"] = arrivals(rng, np.minimum(n, CAP)); return d
def check_inputs(d):
    bad = []; v = d["ring"].astype(np.float32); hc = d["hc"]
    if not ((v >= 0) & (v <= 255) & (v == np.floor(v))).all(): bad.append("ring")
    if not ((d["had"] >= P // 2) & (d["had"] <= 2 * P)).all(): bad.append("had")
    for e in range(R):
        a = hc[:, :, 6 * e:6 * e + 3]; b = hc[:, :, 6 * e + 3:6 * e + 6]
        if not ((a >= 1) & (a <= 4095) & (a & 1 == 1)).all() or not ((b >= 0) & (b <= 4095)).all(): bad.append("hash")
    f = hc[:, :, 6 * R:]
    if not ((f >= 1) & (f <= 255) & (f & 1 == 1)).all(): bad.append("factors")
    if not ((d["came"] == 0) | (d["came"] == 1)).all(): bad.append("flags")
    elif np.max(np.sum(get(d["came"]), axis=-1)) > CAP: bad.append("cap")
    return bad
def reference(ring, had, hc, came):
    y = ring.astype(np.float32).astype(np.int64).reshape(N, 8, 16, P); m = had[:, :, 0].astype(np.int64); h = hc.astype(np.int64)
    fl = get(came) == 1; x = np.arange(N * T)
    for e in range(R):
        pk = np.zeros((N, 8, 16, N * T), np.int64)
        for q in range(N):
            for g in range(8):
                c = min(int(m[q, g]), P)
                for k in range(3):
                    u = (h[q, g, 6 * e + k] * x + h[q, g, 6 * e + 3 + k]) & 4095
                    s = (u * u) & 2047
                    p = (((2 * s + u) & 4095) * c) >> 12
                    pk[q, g] += h[q, g, 6 * R + k] * y[q, g][:, p]
        pk = pk & 255
        for r in range(N):
            for g in range(8):
                for d in range(1, N):
                    keep = pk[(r + d) % N, g][:, r * T:r * T + T][:, fl[r, g, e, d - 1]]; n = keep.shape[1]
                    y[r, g][:, (m[r, g] + np.arange(n)) & (P - 1)] = keep
                    m[r, g] += n
    return {"y": y.reshape(N, 128, P).astype(np.float32), "now": m.reshape(N, 8, 1).astype(np.float32)}

@@ -1,0 +1,445 @@
+from concourse.bass import DstId, RemoteDMATransfer
+from concourse.mybir import AluOpType as A, ActivationFunctionType as AF
+
+N, P, R, CAP = 4, 4096, 4, 256
+HW = 144
+FO = 4 * HW
+ONES, TRI, E1, B1, E2, B2, ID, ID4, IDN, ZERO, BIG, FD, GD = 0, 1, 2, 6, 7, 11, 12, 13, 14, 15, 16, 17, 20
+NMAT = 31
+OPT = {
+    "batches": [[0], [1], [2]],
+    "vset": (6, 7),
+    "chunks": [256, 256, 768, 768, 1024, 1024],
+    "lat": 2500.0, "lats": 3800.0, "first": 2500.0, "ring": 1100.0, "gap": 600.0, "tol": 50.0,
+}
+
+SCRATCH = {"p" + b: ("psum", [128, 512], "float32") for b in "ABCDLMTF"}
+for _dt, _bufs in (("bfloat16", dict(W=P + 12 * CAP, mt=128 * NMAT, iot=512, rst=288, crow=288, F=480, S=480, Bb=480, Rb=480,
+                                     Ps=4 * 480, sg=18 * HW + 12 * 256, G=9 * CAP, out=12 * CAP)),
+                   ("int32", dict(cm=384, fl=96, hh=32, pc=4, z=FO, u=FO, s=FO, pp=FO + 256, ps=FO + 256, q=3 * CAP)),
+                   ("float32", dict(hf=32, C=32, m32=128 * 5, e8=128, o8=128, pf=16, tb=256, jf=FO + 256, sh=FO + 256, Y=P)),
+                   ("uint16", dict(Lo=192, Li=192, L3=48, off=FO + 256))):
+    for _k in _bufs:
+        SCRATCH[_k] = ("sbuf", [128, _bufs[_k]], _dt)
+SEMAPHORES = ["sv", "sa", "sp", "sq", "ld0", "ld1", "ld2", "ld3", "rg0", "rg1", "rg2", "rg3", "al0", "al1", "al2", "afl",
+              "ar0", "ar1", "ar2", "ar3", "sent", "st", "stn"]
+
+CUM, TH, NW, GN, GH, GW, SG, SH, MM, CC, CON, WH, HC, THR = 0, 16, 32, 48, 64, 80, 96, 112, 128, 132, 140, 144, 148, 160
+
+
+def dest_order(cores, q, topo):
+    o = [(q - d) % N for d in range(1, N)]
+    near = lambda r: topo.same_plane(topo.chip(cores[q]), topo.chip(cores[r]))
+    return [r for r in o if not near(r)] + [r for r in o if near(r)]
+
+
+def split_masks(engines):
+    h, k = len(engines) // 2, len(engines) // 4
+    parts = [engines[:h], engines[h:h + k], engines[h + k:h + 2 * k]]
+    return [(sum(1 << e for e in p), len(p)) for p in parts]
+
+
+def arrange(ops):
+    n = len(ops)
+    wr, rd = {}, {}
+    for i, o in enumerate(ops):
+        pre = set(wr[k] for k in o["r"] + o["w"] if k in wr)
+        for k in o["w"]:
+            pre.update(rd.get(k, []))
+        pre.discard(i)
+        o["pre"] = sorted(pre)
+        for k in o["r"]:
+            rd.setdefault(k, []).append(i)
+        for k in o["w"]:
+            wr[k] = i
+            rd[k] = []
+    way = [0.0] * n
+    succ = [[] for _ in ops]
+    for i, o in enumerate(ops):
+        for j in o["pre"]:
+            succ[j].append(i)
+    for i in range(n - 1, -1, -1):
+        way[i] = ops[i]["c"] + ops[i]["l"] + max([way[j] for j in succ[i]] + [0.0])
+    left = [len(o["pre"]) for o in ops]
+    due, free = [0.0] * n, {}
+    pool = [i for i in range(n) if not left[i]]
+    order, done = [], set()
+    while pool:
+        t0, e = min((max(due[i], free.get(ops[i]["e"], 0.0)), i) for i in pool)
+        e = ops[e]["e"]
+        est, soon, top = {}, [], 0.0
+        for k in range(n):
+            if k in done:
+                continue
+            t = max(due[k], free.get(ops[k]["e"], 0.0), t0)
+            for j in ops[k]["pre"]:
+                if j not in done:
+                    t = max(t, est[j] + ops[j]["c"] + ops[j]["l"])
+            est[k] = t
+            top = max(top, t + way[k])
+            if ops[k]["e"] == e and t < t0 + 1200.0:
+                soon.append(k)
+        i = None
+        for k in sorted((k for k in pool if ops[k]["e"] == e and due[k] <= t0 + 1e-6), key=lambda k: (-way[k], k)):
+            end = t0 + ops[k]["c"]
+            if all(way[m] <= way[k] or end + way[m] <= top + OPT["tol"] or end - est[m] <= OPT["tol"] for m in soon):
+                i = k
+                break
+        if i is None:
+            free[e] = max(t0 + 20.0, min([est[m] for m in soon if est[m] > t0] or [0.0]))
+            continue
+        done.add(i)
+        pool.remove(i)
+        if e != "x":
+            free[e] = t0 + ops[i]["c"]
+        order.append(i)
+        for j in succ[i]:
+            same = e == "p" and ops[j]["e"] == "p"
+            due[j] = max(due[j], t0 + ops[i]["c"] + (0.0 if same else ops[i]["l"]))
+            left[j] -= 1
+            if not left[j]:
+                pool.append(j)
+    return order
+
+
+def rank_program(g, core, T, topo):
+    rank = T.rank_of(core)
+    if rank is None:
+        return
+    cores = list(T.cores)
+    sem, tb = T.sem, T.tb
+    ops = []
+
+    def op(e, fn, r, w, c, l=80.0, tok=None):
+        ops.append({"e": e, "fn": fn, "r": list(r), "w": list(w), "c": c, "l": l, "tok": tok})
+
+    def cyc(n):
+        return max(64, n) * 1.04
+
+    def mms(bank, items):
+        for i, (o, l, r_, reads, n) in enumerate(items):
+            op("p", lambda o=o, l=l, r_=r_, a=i == 0, b=i == len(items) - 1: g.tensor.matmul(o, l, r_, a, b), reads, [bank], max(64, n) * 0.6)
+
+    def ts(out, in0, s1, s2, o0, o1, r, w, n=64):
+        if o1 is None:
+            op("v", lambda: g.vector.tensor_scalar(out, in0, s1, None, o0), r, w, cyc(n))
+        else:
+            op("v", lambda: g.vector.tensor_scalar(out, in0, s1, s2, o0, o1), r, w, cyc(n))
+
+    def tt(out, a, b, o, r, w, n=64):
+        op("v", lambda: g.vector.tensor_tensor(out, a, b, o), r, w, cyc(n))
+
+    def cp(out, a, r, w, n=64):
+        op("v", lambda: g.vector.tensor_copy(out, a), r, w, cyc(n))
+
+    def scan(out, a, b, r, w, n=64):
+        op("v", lambda: g.vector.tensor_tensor_scan(out, a, b, 0.0, A.mult, A.add), r, w, cyc(n))
+
+    def fill(out, v, w, n=64):
+        op("v", lambda: g.vector.memset(out, v), [], w, cyc(n))
+
+    def act(out, a, f, r, w, n=128, **kw):
+        op("a", lambda: g.scalar.activation(out, a, f, **kw), r, w, cyc(n) + 80)
+
+    def iota(out, pat, base, cmul, key, n, **kw):
+        op("g", lambda: g.iota(out, pat, base, cmul, **kw), [], [key], 160 + 2.1 * n)
+
+    def dma(e, out, src, r, w, name, val, l):
+        q = g.sync if e == "s" else g.scalar
+        op(e, lambda: q.dma_start(out, src).then_inc(sem[name], 16), r, w, 60.0, l, (name, val))
+
+    def mat(i):
+        return T.mt[:, 128 * i:128 * (i + 1)]
+
+    def mk(i):
+        return "m%d" % i
+
+    def col(buf, c):
+        return buf[:, c:c + 1]
+
+    dma("s", T.cm[:, 0:96], T.came[:, 0:96], [], ["cm0"], "ld0", 16, 2100.0)
+    dma("s", T.cm[:, 288:384], T.came[:, 288:384], [], ["cm3"], "ld3", 16, 2200.0)
+    dma("s", T.cm[:, 96:288], T.came[:, 96:288], [], ["cm1", "cm2"], "ld1", 16, 2500.0)
+    dma("a", T.hh[0:8, 0:27], T.hc[:], [], ["hh0"], "ld2", 32, 2100.0)
+    dma("a", T.hh[0:8, 27:28], T.had[:], [], ["hh1"], "ld2", 32, 2100.0)
+    for k in range(4):
+        dma("s", T.W[:, 1024 * k:1024 * (k + 1)], T.ring[:, 1024 * k:1024 * (k + 1)], [], ["W%d" % k], "rg%d" % k, 16,
+            2500.0 + OPT["ring"] * (k + 1))
+    nload = len(ops)
+
+    small = {"allow_small_or_imprecise_dtypes": True}
+    iota(T.pc[:, 0:1], [[0, 1]], 0, 1, "pc0", 1)
+    iota(T.iot[:, 384:512], [[16, 8], [0, 16]], 0, 0, "io3", 128, **small)
+    iota(T.iot[:, 0:128], [[1, 128]], 0, 0, "io0", 128, **small)
+    iota(T.iot[:, 128:256], [[4, 32], [0, 4]], 0, 0, "io1", 128, **small)
+    iota(T.iot[:, 256:384], [[16, 8], [0, 4], [1, 4]], 0, 0, "io2", 128, **small)
+    fill(T.rst[:], 1.0, ["rst"], 144)
+    fill(T.rst[:, 0:288:32], 0.0, ["rst"])
+    fill(mat(ZERO), 0.0, [mk(ZERO)])
+    fill(T.o8[0:8, :], 1.0, ["o8"], 128)
+    fill(col(tb, CUM), 0.0, ["cum0"])
+    for c, m in ((1, 124), (2, 115), (3, 112)):
+        ts(col(T.pc, c), col(T.pc, 0), m, None, A.bitwise_and, None, ["pc0"], ["pc%d" % c])
+    cp(T.pf[:, 0:4], T.pc[:, 0:4], ["pc0", "pc1", "pc2", "pc3"], ["pf"])
+    ts(mat(ONES), T.iot[:, 384:512], col(T.pf, 3), None, A.is_equal, None, ["io3", "pf"], [mk(ONES)])
+    ts(mat(ID), T.iot[:, 0:128], col(T.pf, 0), None, A.is_equal, None, ["io0", "pf"], [mk(ID)])
+    ts(mat(TRI), T.iot[:, 0:128], col(T.pf, 0), -1.0, A.is_lt, A.mult, ["io0", "pf"], [mk(TRI)])
+    tt(mat(TRI), mat(TRI), mat(ONES), A.mult, [mk(TRI), mk(ONES)], [mk(TRI)], 128)
+    for a in range(4):
+        ts(mat(E1 + a), T.iot[:, 0:128], col(T.pf, 1), float(a), A.subtract, A.is_equal, ["io0", "pf"], [mk(E1 + a)])
+        ts(mat(E2 + a), T.iot[:, 0:128], col(T.pf, 2), float(4 * a), A.subtract, A.is_equal, ["io0", "pf"], [mk(E2 + a)])
+    ts(mat(B1), T.iot[:, 128:256], col(T.pf, 1), 0.25, A.is_equal, A.mult, ["io1", "pf"], [mk(B1)])
+    ts(mat(B2), T.iot[:, 256:384], col(T.pf, 2), 0.25, A.is_equal, A.mult, ["io2", "pf"], [mk(B2)])
+    iota(T.crow[:], [[512, 4], [0, 72]], 512, 0, "crow", 288, **small)
+    op("g", lambda: g.affine_select(T.e8[0:8, :], T.o8[0:8, :], [[1, 8], [0, 16]], A.is_equal, 0.0, 0, -1), ["o8"], ["e8"], 480.0)
+    iota(T.ps[:, FO:FO + 256], [[16, 256]], -2047, 1, "ps4", 256)
+    for i, sc in ((ID4, 0.25), (IDN, -1.0), (BIG, 8192.0)):
+        act(mat(i), mat(ID), AF.Copy, [mk(ID)], [mk(i)], scale=sc)
+    act(T.m32[:, 0:128], mat(ID), AF.Copy, [mk(ID)], ["i32"])
+
+    def flags(src, lo, n, r, key):
+        cp(T.F[:, lo:lo + n], src, r, ["F" + key], n)
+        scan(T.S[:, lo:lo + n], T.rst[:, 0:n], T.F[:, lo:lo + n], ["rst", "F" + key], ["S" + key], n // 2)
+
+    def lists(lo, nb, key, b0, b1):
+        n = 32 * nb
+        Bb, Rb = T.Bb[:, lo:lo + n], T.Rb[:, lo:lo + n]
+        pl = 4 * lo
+        kb, kr = "Bb" + key, "Rb" + key
+        kp = ["Ps%s_%d" % (key, a) for a in range(4)]
+        ps = lambda a: T.Ps[:, pl + a * n:pl + (a + 1) * n]
+
+        def split(bank, h):
+            m = 1.5 * 2 ** 23 * 4 * h
+            V = T[bank][:, 0:n]
+            ts(Bb, V, m, m, A.add, A.subtract, [bank], [kb], n)
+            tt(Rb, V, Bb, A.subtract, [bank, kb], [kr], n)
+            h = float(h)
+            for a, (s1, s2, o0, o1) in enumerate(((0.0, h, A.max, A.min), (-h, 0.0, A.add, A.max),
+                                                  (h, 0.0, A.add, A.min), (-h, 0.0, A.max, A.min))):
+                ts(ps(a), Rb, s1, s2, o0, o1, [kr], [kp[a]], n // 2)
+
+        mms(b0, [(T[b0][:, 0:n], mat(TRI), T.F[:, lo:lo + n], ["F" + key, mk(TRI)], n),
+                 (T[b0][:, 0:n], mat(ONES), T.S[:, lo:lo + n], ["S" + key, mk(ONES)], n)])
+        for src, dst, h, eb, bb in ((b0, b1, 1, E1, B1), (b1, b0, 4, E2, B2)):
+            split(src, h)
+            mms(dst, [(T[dst][:, 0:n], mat(bb), Bb, [kb, mk(bb)], n)] +
+                [(T[dst][:, 0:n], mat(eb + a), ps(a), [kp[a], mk(eb + a)], n) for a in range(4)])
+        split(b0, 16)
+        k = n // 4
+        mms(b1, [(T[b1][:, 0:n], mat(ZERO), Bb, [kb, mk(ZERO)], n)] +
+            [(T[b1][:, a * k:(a + 1) * k], mat(ID4), T.Bb[:, lo + c:lo + n:4], [kb, mk(ID4)], k) for a in range(4) for c in range(4)] +
+            [(T[b1][:, 0:n], mat(ID), T.Ps[:, pl + c:pl + 4 * n:4], kp + [mk(ID)], n) for c in range(4)])
+        if nb > 3:
+            cp(Rb, T[b1][:, 0:n], [b1], [kr], n)
+        for a in range(4):
+            if nb > 3:
+                ts(ps(a), Rb, 64.0 * a, 64.0 * a + 64.0, A.max, A.min, [kr], [kp[a]], n // 2)
+            else:
+                ts(ps(a), T[b1][:, 0:n], 64.0 * a, 64.0 * a + 64.0, A.max, A.min, [b1], [kp[a]], n)
+        w = 16 * nb
+        mms(b0, [(T[b0][:, 0:w], mat(ID), T.crow[:, 0:288:18 // nb], ["crow", mk(ID)], w)] +
+            [(T[b0][:, 0:w], mat(IDN), T.Ps[:, pl + c:pl + 4 * n:8], kp + [mk(IDN)], w) for c in range(8)])
+
+    sent = [0]
+    order = dest_order(cores, rank, topo)
+    masks = split_masks(topo.engines(core, cores[(rank + 1) % N]))
+    nmask = sum(m[1] for m in masks)
+
+    def to_makers(src, dst, name, r, w, after):
+        trs = []
+        for d in range(1, N):
+            q = (rank + d) % N
+            rid, pid, _ = topo.addr(cores[q])
+            pos = dest_order(cores, q, topo).index(rank)
+            trs.append(RemoteDMATransfer(dst_ids=[DstId(rid=rid, pnc=pid)], dma_engine_mask=masks[d - 1][0], remote_sem=sem[name],
+                                         src=src(d - 1), dst=dst(pos)))
+        op("g", lambda: g.remote_dma_fused(trs, local_sem=sem.sent), r, ["x" + name, "gq"], 300.0, 0.0, ("", 0))
+        sent[0] += nmask
+        op("x", None, ["x" + name], w, 0.0, after, (name, nmask))
+
+    xs = {}
+    to_makers(lambda d: T.cm[:, 288 + 32 * d:320 + 32 * d], lambda p: T.fl[:, 32 * p:32 * p + 32], "afl", ["cm3"], ["fl"],
+              OPT["lats"] + OPT["first"])
+    banks = [("pL", "pM"), ("pD", "pC"), ("pL", "pM")]
+    for i, rounds in enumerate(OPT["batches"]):
+        e0, ne = rounds[0], len(rounds)
+        key = str(e0)
+        flags(T.cm[:, 96 * e0:96 * (e0 + ne)], 96 * e0, 96 * ne, ["cm%d" % e for e in rounds], key)
+        lists(96 * e0, 3 * ne, key, *banks[i])
+        k, o = 16 * ne, 48 * e0
+        for d in range(3):
+            ts(T.Lo[:, o + d * k:o + (d + 1) * k], T[banks[i][0]][:, d:3 * k:3], 512.0 * rank, None, A.add, None, [banks[i][0]], ["Lo%s_%d" % (key, d)])
+        to_makers(lambda d, o=o, k=k: T.Lo[:, o + d * k:o + (d + 1) * k], lambda p, o=o, k=k: T.Li[:, o + p * k:o + (p + 1) * k],
+                  "al%d" % i, ["Lo%s_%d" % (key, d) for d in range(3)], ["Li" + key], OPT["lats"])
+        for e in rounds:
+            xs[e] = (T.Li[:, o + e - e0:o + 3 * k:ne], ["Li" + key])
+    flags(T.cm[:, 288:384], 288, 96, ["cm3"], "3")
+    flags(T.fl[:], 384, 96, ["fl"], "4")
+    lists(384, 3, "4", "pL", "pM")
+    for p in range(3):
+        ts(T.L3[:, 16 * p:16 * p + 16], T.pL[:, p:48:3], 512.0 * order[p], None, A.add, None, ["pL"], ["L3_%d" % p])
+    xs[3] = (T.L3[:], ["L3_0", "L3_1", "L3_2"])
+
+    for k in range(4):
+        sl = T.W[:, 1024 * k:1024 * (k + 1)]
+        act(sl, sl, AF.Copy, ["W%d" % k], ["W%d" % k], 1024, scale=1.0 / 256)
+
+    ts(T.hh[0:8, 28:29], T.hh[0:8, 27:28], 4095, None, A.bitwise_and, None, ["hh0", "hh1"], ["hh2"])
+    cp(T.hf[0:8, 0:29], T.hh[0:8, 0:29], ["hh0", "hh1", "hh2"], ["hf"])
+    mms("pT", [(T.pT[:, 0:29], T.e8[0:8, :], T.hf[0:8, 0:29], ["e8", "hf"], 256)])
+    cp(T.C[:, 0:29], T.pT[:, 0:29], ["pT"], ["C"])
+    mms("pF", [(T.pF[:, 0:12], mat(ONES), T.S[:, 31:384:32], ["S%d" % b[0] for b in OPT["batches"]] + ["S3", mk(ONES)], 64)])
+    for k in range(3):
+        act(mat(FD + k), mat(ID), AF.Copy, [mk(ID), "C"], [mk(FD + k)], scale=col(T.C, 24 + k))
+    had, h0 = col(T.C, 27), col(T.C, 28)
+    t12 = lambda c: tb[:, c:c + 12]
+    t13 = lambda c: tb[:, c:c + 13]
+    t4 = lambda c: tb[:, c:c + 4]
+    ts(col(tb, CC), had, 4096.0, 1.0 / 4096, A.min, A.mult, ["C"], ["cc0"])
+    scan(t12(CUM + 1), T.rst[:, 1:13], T.pF[:, 0:12], ["rst", "pF"], ["cum"])
+    ts(t12(GN), T.pF[:, 0:12], -256.0, None, A.add, None, ["pF"], ["gn"])
+    ts(t12(GH), T.pF[:, 0:12], -256.0, 0.5, A.add, A.mult, ["pF"], ["gh"])
+    ts(t4(MM), tb[:, CUM + 3:CUM + 13:3], had, None, A.add, None, ["cum", "C"], ["mm"])
+    ts(t4(CC + 1), t4(MM), 4096.0, 1.0 / 4096, A.min, A.mult, ["mm"], ["cc1"])
+    dma("s", T.now[:], tb[0:128:16, MM + 3:MM + 4], ["mm"], ["now"], "stn", 16, 2000.0)
+    ts(t13(TH), t13(CUM), h0, None, A.add, None, ["cum0", "cum", "C"], ["th"])
+    ts(t13(NW), t13(TH), 4096.0, None, A.is_lt, None, ["th"], ["nw"])
+    ts(t13(GW), t13(TH), 4096.0, -4096.0, A.is_ge, A.mult, ["th"], ["gw"])
+    tt(t13(TH), t13(TH), t13(GW), A.add, ["th", "gw"], ["th"])
+    tt(t12(GW), t12(GN), t12(NW + 1), A.mult, ["gn", "nw"], ["gw"])
+    scan(t12(SG), T.rst[:, 1:13], t12(GW), ["rst", "gw"], ["sg"])
+    scan(t12(SH), T.rst[:, 1:13], t12(GH), ["rst", "gh"], ["sh"])
+    ts(col(tb, HC), h0, -1.0, 6144.0, A.mult, A.add, ["C"], ["hc"])
+    ts(t4(CON), tb[:, NW + 3:NW + 13:3], -16384.0, col(tb, HC), A.mult, A.add, ["nw", "hc"], ["con"])
+    tt(t4(CON), t4(CON), tb[:, SG + 1:SG + 12:3], A.subtract, ["con", "sg"], ["con"])
+    ts(t4(WH), tb[:, SH + 1:SH + 12:3], -1.0, -6144.0, A.mult, A.add, ["sh"], ["wh"])
+    for e in range(1, 5):
+        o = THR + 16 * (e - 1)
+        ts(tb[:, o:o + 3 * e + 1], tb[:, TH:TH + 3 * e + 1], col(tb, CON + e - 1), -2047.5, A.add, A.add, ["th", "con"], ["thr%d" % e])
+        act(T.m32[:, 128 * e:128 * (e + 1)], mat(ID), AF.Copy, [mk(ID), "wh"], ["w32%d" % e], scale=col(tb, WH + e - 1))
+    for b in range(11):
+        act(mat(GD + b), mat(ID), AF.Copy, [mk(ID), "gn", "gh"], [mk(GD + b)], scale=col(tb, (GN if b in OPT["vset"] else GH) + b))
+
+    def places(e):
+        x, xk = xs[e]
+        o = e * HW
+        zs = ["z%d_%d" % (e, k) for k in range(3)]
+        z, u, s = T.z[:, o:o + HW], T.u[:, o:o + HW], T.s[:, o:o + HW]
+        ku, ks = "u%d" % e, "s%d" % e
+        for k in range(3):
+            ts(T.z[:, o + 48 * k:o + 48 * (k + 1)], x, col(T.C, 6 * e + k), col(T.C, 6 * e + 3 + k), A.mult, A.add, xk + ["C"], [zs[k]])
+        ts(u, z, 4095, None, A.bitwise_and, None, zs, [ku], HW)
+        ts(s, u, 2.0, -4095.0, A.mult, A.add, [ku], [ks], HW)
+        tt(z, u, s, A.mult, [ku, ks], zs, 2 * HW)
+        ts(u, z, 4095, None, A.bitwise_and, None, zs, [ku], HW)
+        if e == 0:
+            ts(T.pp[:, 0:HW], u, col(tb, CC), -2047.5 + 2.0 ** -13, A.mult, A.add, [ku, "cc0"], ["pp0"], HW)
+            ts(T.off[:, 0:HW], T.pp[:, 0:HW], 2047.0, None, A.add, None, ["pp0"], ["off0"], HW)
+        else:
+            ts(T.pp[:, o:o + HW], u, col(tb, CC + e), -2047.5 + 2.0 ** -13, A.mult, A.add, [ku, "cc1"], ["pp%d" % e], HW)
+            positions(e)
+
+    def positions(e):
+        o, n, bank = (e * HW, HW, "pT") if e < 4 else (FO, 256, "pF")
+        pp, jf, kp, kj = T.pp[:, o:o + n], T.jf[:, o:o + n], "pp%d" % e, "jf%d" % e
+        nb, th, kt = 3 * e, THR + 16 * (e - 1), "thr%d" % e
+        so = HW * (3 * e * (e - 1) // 2)
+        ts(jf, pp, col(tb, CON + e - 1), None, A.add, None, [kp, "con"], [kj], n)
+        act(T.sh[:, o:o + n], jf, AF.Sign, [kj, kt], ["sh%d" % e], n, bias=col(tb, th), scale=-1.0)
+        X = T[bank][:, 0:n]
+        items = [(X, T.m32[:, 0:128], jf, ["i32", kj], 4 * n),
+                 (X, T.m32[:, 128 * e:128 * (e + 1)], T.sh[:, o:o + n], ["w32%d" % e, "sh%d" % e], 4 * n)]
+        for b in range(nb):
+            sl, k = T.sg[:, so + b * n:so + (b + 1) * n], "sg%d_%d" % (e, b)
+            if b in OPT["vset"] and b < nb - 1:
+                ts(sl, jf, col(tb, th + 1 + b), -0.5, A.is_lt, A.add, [kj, kt], [k], n)
+            else:
+                act(sl, jf, AF.Sign, [kj, kt], [k], n, bias=col(tb, th + 1 + b), scale=-1.0)
+            m = BIG if b == nb - 1 else GD + b
+            items.append((X, mat(m), sl, [k, mk(m)], n))
+        mms(bank, items)
+        tt(T.ps[:, o:o + n], X, pp, A.max, [bank, kp], ["ps%d" % e], n)
+        ts(T.off[:, o:o + n], T.ps[:, o:o + n], 2047.0, None, A.add, None, ["ps%d" % e], ["off%d" % e], n)
+
+    def window(e):
+        return T.W[:, 0:P + 3 * CAP * e], ["W0", "W1", "W2", "W3"] + ["land%d" % i for i in range(e)]
+
+    def make(e):
+        win, wk = window(e)
+        for j in range(3):
+            bank = "p" + "ABC"[j]
+            x, qq, o = T[bank][:, 0:CAP], T.q[:, j * CAP:(j + 1) * CAP], T.out[:, (3 * e + j) * CAP:(3 * e + j + 1) * CAP]
+            items = []
+            for k in (2, 0, 1):
+                c = e * HW + 48 * k + 16 * j
+                src = win.indirect(T.off[:, c:c + 16])
+                dst, key = T.G[:, (3 * j + k) * CAP:(3 * j + k + 1) * CAP], "G%d_%d" % (j, k)
+                if k < 2:
+                    act(dst, src, AF.Copy, wk + ["off%d" % e], [key], 1.56 * CAP)
+                else:
+                    cp(dst, src, wk + ["off%d" % e], [key], 1.56 * CAP + 60)
+                items.append((x, mat(FD + k), dst, [key, mk(FD + k)], CAP))
+            mms(bank, items)
+            ts(qq, x, -127.5 / 256, None, A.add, None, [bank], ["q%d" % j], CAP)
+            tt(o, x, qq, A.subtract, [bank, "q%d" % j], ["o%d" % (3 * e + j)], CAP)
+            r = order[j]
+            rid, pid, _ = topo.addr(cores[r])
+            c = P + (3 * e + (rank - r) % N - 1) * CAP
+            op("g", lambda c=c, o=o, r=r, pid=pid, rid=rid: g.remote_dma(T.W[:, c:c + CAP], o, sem["ar%d" % e], sem.sent, pid, rid,
+                                                                         topo.mask(core, cores[r])),
+               ["o%d" % (3 * e + j)], ["x%d_%d" % (e, j), "gq"], 300.0, OPT["gap"] * (2 - j), ("", 0))
+            sent[0] += len(topo.engines(core, cores[r]))
+        op("x", None, ["x%d_%d" % (e, j) for j in range(3)], ["land%d" % e], 0.0, OPT["lat"],
+           ("ar%d" % e, sum(len(topo.engines(cores[q], core)) for q in range(N) if q != rank)))
+
+    for e in range(4):
+        places(e)
+        make(e)
+    ts(T.pp[:, FO:FO + 256], T.ps[:, FO:FO + 256], col(T.pf, 3), None, A.subtract, None, ["ps4", "pf"], ["pp4"], 256)
+    positions(4)
+
+    win, wk = window(4)
+    c = 0
+    for i, n in enumerate(OPT["chunks"]):
+        src = win.indirect(T.off[:, FO + c // 16:FO + (c + n) // 16])
+        dst = T.Y[:, c:c + n]
+        if i % 2:
+            act(dst, src, AF.Copy, wk + ["off4"], ["Y%d" % i], 1.56 * n, scale=256.0)
+        else:
+            ts(dst, src, 256.0, None, A.mult, None, wk + ["off4"], ["Y%d" % i], 1.56 * n)
+        dma("s", T.y[:, c:c + n], dst, ["Y%d" % i], ["yq"], "st", 0, 3.0 * n)
+        c += n
+
+    Q = {"v": g.vector, "a": g.scalar, "p": g.tensor, "g": g, "s": g.sync}
+    own = {"v": "sv", "a": "sa", "p": "sp", "g": "sq"}
+    cnt = {"sv": 0, "sa": 0, "sp": 0, "sq": 0}
+    waited = {k: {} for k in Q}
+
+    def wait(e, name, val):
+        if name and waited[e].get(name, 0) < val:
+            Q[e].wait_ge(sem[name], val)
+            waited[e][name] = val
+
+    for i in list(range(nload)) + [i for i in arrange(ops) if i >= nload]:
+        o = ops[i]
+        e = o["e"]
+        if e == "x":
+            continue
+        need = {}
+        for j in o["pre"]:
+            name, val = ops[j]["tok"]
+            if not (e == "p" and name == "sp"):
+                need[name] = max(need.get(name, 0), val)
+        for name in need:
+            wait(e, name, need[name])
+        ins = o["fn"]()
+        if o["tok"] is None:
+            cnt[own[e]] += 1
+            ins.then_inc(sem[own[e]], 1)
+            o["tok"] = (own[e], cnt[own[e]])
+    for name in cnt:
+        wait("g", name, cnt[name])
+    wait("g", "sent", sent[0])
+    wait("s", "stn", 16)
+    wait("s", "st", 16 * len(OPT["chunks"]))

@@ -4,27 +4,31 @@ from concourse.mybir import AluOpType as A, ActivationFunctionType as AF
 N, P, R, CAP = 4, 4096, 4, 256
 HW = 144
 FO = 4 * HW
-ONES, TRI, E1, B1, E2, B2, ID, ID4, IDN, ZERO, BIG, FD, GD = 0, 1, 2, 6, 7, 11, 12, 13, 14, 15, 16, 17, 20
-NMAT = 31
+ONES, TRI, E1, E2, B2, ID, ID4, IDN, FD, HALF, GD = 0, 1, 2, 6, 10, 11, 12, 13, 14, 17, 18
+NMAT = 29
 OPT = {
-    "batches": [[0], [1], [2]],
-    "vset": (6, 7),
-    "chunks": [256, 256, 768, 768, 1024, 1024],
-    "lat": 2500.0, "lats": 3800.0, "first": 2500.0, "ring": 1100.0, "gap": 600.0, "tol": 50.0,
+    "raw": [3],
+    "batches": [[0], [1, 2]],
+    "multi": True, "passes": 3, "tol": 40.0,
+    "ring": 2, "scale": "aavvaavv", "l1": {"0": 1, "1": 4, "4": 4}, "dup": {"0": 2, "1": 2, "4": 1}, "hsplit": 1, "signs": [1, 2], "cuts": [[256], [256], [192, 64]],
+    "vg": [(0, 2, 0), (1, 2, 0), (1, 0, 0), (2, 2, 1)],
+    "chunks": [256, 512, 640, 640],
+    "lat": 2500.0, "lats": 3000.0, "first": 1500.0, "load": 3000.0, "gap": 500.0, "wake": 80.0,
 }
 
 SCRATCH = {"p" + b: ("psum", [128, 512], "float32") for b in "ABCDLMTF"}
-for _dt, _bufs in (("bfloat16", dict(W=P + 12 * CAP, mt=128 * NMAT, iot=512, rst=288, crow=288, F=480, S=480, Bb=480, Rb=480,
-                                     Ps=4 * 480, sg=18 * HW + 12 * 256, G=9 * CAP, out=12 * CAP)),
-                   ("int32", dict(cm=384, fl=96, hh=32, pc=4, z=FO, u=FO, s=FO, pp=FO + 256, ps=FO + 256, q=3 * CAP)),
-                   ("float32", dict(hf=32, C=32, m32=128 * 5, e8=128, o8=128, pf=16, tb=256, jf=FO + 256, sh=FO + 256, Y=P)),
-                   ("uint16", dict(Lo=192, Li=192, L3=48, off=FO + 256))):
+for _dt, _bufs in (("bfloat16", dict(W=P + 12 * CAP, mt=128 * NMAT, iot=384, rst=288, crow=144, cb=288, F=672, S=672, Bb=1344, Rb=672,
+                                     Ps=4 * 672, sg=18 * HW + 12 * 256, G=9 * CAP, out=12 * CAP)),
+                   ("float16", dict(jh=FO + 256, i16=128)),
+                   ("int32", dict(cm=384, fl=288, hh=32, pc=4, z=FO, u=FO, pp=FO, q=3 * CAP)),
+                   ("float32", dict(hf=32, C=32, i32=128, e8=128, o8=128, pf=16, tb=160, j0=256, jf=FO, m32=512, big=2 * (FO + 256), Y=P)),
+                   ("uint16", dict(Lo=192, Li=640, L3=144, off=FO + 256))):
     for _k in _bufs:
         SCRATCH[_k] = ("sbuf", [128, _bufs[_k]], _dt)
 SEMAPHORES = ["sv", "sa", "sp", "sq", "ld0", "ld1", "ld2", "ld3", "rg0", "rg1", "rg2", "rg3", "al0", "al1", "al2", "afl",
               "ar0", "ar1", "ar2", "ar3", "sent", "st", "stn"]
 
-CUM, TH, NW, GN, GH, GW, SG, SH, MM, CC, CON, WH, HC, THR = 0, 16, 32, 48, 64, 80, 96, 112, 128, 132, 140, 144, 148, 160
+THR, MR, NG, WR, TH, SH, XU, ZU, CC, WE, KK, NW, H2, ZC, KS = 0, 16, 32, 48, 64, 80, 96, 112, 128, 132, 136, 140, 141, 142, 144
 
 
 def dest_order(cores, q, topo):
@@ -39,6 +43,47 @@ def split_masks(engines):
     return [(sum(1 << e for e in p), len(p)) for p in parts]
 
 
+def sweep(ops, before, after, lag, due, late):
+    n = len(ops)
+    left = [len(before[i]) for i in range(n)]
+    start, free, todo = [None] * n, {}, {}
+    for i in sorted(range(n), key=lambda i: (late[i], i)):
+        todo.setdefault(ops[i]["e"], []).append(i)
+        free[ops[i]["e"]] = 0.0
+    pool = set(i for i in range(n) if not left[i])
+
+    def soonest(i, t, memo):
+        if i not in memo:
+            memo[i] = max([due[i], t, free[ops[i]["e"]]] +
+                          [soonest(j, t, memo) + ops[j]["c"] + lag(j, i) for j in before[i] if start[j] is None])
+        return memo[i]
+
+    shift = 0.0
+    while pool:
+        t, e = min((max(due[i], free[ops[i]["e"]]), ops[i]["e"]) for i in pool)
+        memo, pick, ahead = {}, None, []
+        for i in todo[e][:40]:
+            if i in pool and due[i] <= t + 1e-6 and all(t + ops[i]["c"] <= max(s, late[m] + shift) + OPT["tol"] for m, s in ahead):
+                pick = i
+                break
+            ahead.append((i, soonest(i, t, memo)))
+        if pick is None:
+            free[e] = min([s for m, s in ahead if s > t + 1e-6] or [t + 20.0])
+            continue
+        start[pick] = t
+        shift = max(shift, t - late[pick])
+        todo[e].remove(pick)
+        pool.remove(pick)
+        if e != "x":
+            free[e] = t + ops[pick]["c"]
+        for j in after[pick]:
+            due[j] = max(due[j], t + ops[pick]["c"] + lag(pick, j))
+            left[j] -= 1
+            if not left[j]:
+                pool.add(j)
+    return start
+
+
 def arrange(ops):
     n = len(ops)
     wr, rd = {}, {}
@@ -46,6 +91,9 @@ def arrange(ops):
         pre = set(wr[k] for k in o["r"] + o["w"] if k in wr)
         for k in o["w"]:
             pre.update(rd.get(k, []))
+        for k in o["r"]:
+            if k in SCRATCH and SCRATCH[k][0] == "psum":
+                pre.update(j for j in rd.get(k, []) if ops[j]["e"] != o["e"])
         pre.discard(i)
         o["pre"] = sorted(pre)
         for k in o["r"]:
@@ -53,53 +101,28 @@ def arrange(ops):
         for k in o["w"]:
             wr[k] = i
             rd[k] = []
-    way = [0.0] * n
     succ = [[] for _ in ops]
     for i, o in enumerate(ops):
         for j in o["pre"]:
             succ[j].append(i)
+    lag = lambda i, j: 0.0 if ops[i]["e"] == ops[j]["e"] == "p" else ops[i]["l"]
+
+    pre = [o["pre"] for o in ops]
+    way = [0.0] * n
     for i in range(n - 1, -1, -1):
-        way[i] = ops[i]["c"] + ops[i]["l"] + max([way[j] for j in succ[i]] + [0.0])
-    left = [len(o["pre"]) for o in ops]
-    due, free = [0.0] * n, {}
-    pool = [i for i in range(n) if not left[i]]
-    order, done = [], set()
-    while pool:
-        t0, e = min((max(due[i], free.get(ops[i]["e"], 0.0)), i) for i in pool)
-        e = ops[e]["e"]
-        est, soon, top = {}, [], 0.0
-        for k in range(n):
-            if k in done:
-                continue
-            t = max(due[k], free.get(ops[k]["e"], 0.0), t0)
-            for j in ops[k]["pre"]:
-                if j not in done:
-                    t = max(t, est[j] + ops[j]["c"] + ops[j]["l"])
-            est[k] = t
-            top = max(top, t + way[k])
-            if ops[k]["e"] == e and t < t0 + 1200.0:
-                soon.append(k)
-        i = None
-        for k in sorted((k for k in pool if ops[k]["e"] == e and due[k] <= t0 + 1e-6), key=lambda k: (-way[k], k)):
-            end = t0 + ops[k]["c"]
-            if all(way[m] <= way[k] or end + way[m] <= top + OPT["tol"] or end - est[m] <= OPT["tol"] for m in soon):
-                i = k
-                break
-        if i is None:
-            free[e] = max(t0 + 20.0, min([est[m] for m in soon if est[m] > t0] or [0.0]))
-            continue
-        done.add(i)
-        pool.remove(i)
-        if e != "x":
-            free[e] = t0 + ops[i]["c"]
-        order.append(i)
-        for j in succ[i]:
-            same = e == "p" and ops[j]["e"] == "p"
-            due[j] = max(due[j], t0 + ops[i]["c"] + (0.0 if same else ops[i]["l"]))
-            left[j] -= 1
-            if not left[j]:
-                pool.append(j)
-    return order
+        way[i] = ops[i]["c"] + max([lag(i, j) + way[j] for j in succ[i]] or [ops[i]["l"]])
+    late = [max(way) - w for w in way]
+    best = None
+    for _ in range(OPT["passes"] + 1):
+        start = sweep(ops, pre, succ, lag, [0.0] * n, late)
+        span = max(start[i] + ops[i]["c"] + ops[i]["l"] for i in range(n))
+        if best is None or span < best[0]:
+            best = (span, start)
+        back = sweep(ops, succ, pre, lambda i, j: lag(j, i), [0.0 if succ[i] else ops[i]["l"] for i in range(n)],
+                     [span - start[i] - ops[i]["c"] for i in range(n)])
+        top = max(back[i] + ops[i]["c"] for i in range(n))
+        late = [top - back[i] - ops[i]["c"] for i in range(n)]
+    return sorted(range(n), key=lambda i: (best[1][i], i))
 
 
 def rank_program(g, core, T, topo):
@@ -110,7 +133,7 @@ def rank_program(g, core, T, topo):
     sem, tb = T.sem, T.tb
     ops = []
 
-    def op(e, fn, r, w, c, l=80.0, tok=None):
+    def op(e, fn, r, w, c, l=OPT["wake"], tok=None):
         ops.append({"e": e, "fn": fn, "r": list(r), "w": list(w), "c": c, "l": l, "tok": tok})
 
     def cyc(n):
@@ -118,7 +141,7 @@ def rank_program(g, core, T, topo):
 
     def mms(bank, items):
         for i, (o, l, r_, reads, n) in enumerate(items):
-            op("p", lambda o=o, l=l, r_=r_, a=i == 0, b=i == len(items) - 1: g.tensor.matmul(o, l, r_, a, b), reads, [bank], max(64, n) * 0.6)
+            op("p", lambda o=o, l=l, r_=r_, a=i == 0, b=i == len(items) - 1: g.tensor.matmul(o, l, r_, a, b), reads, [bank], 20 + max(64, n) * 0.52)
 
     def ts(out, in0, s1, s2, o0, o1, r, w, n=64):
         if o1 is None:
@@ -132,14 +155,14 @@ def rank_program(g, core, T, topo):
     def cp(out, a, r, w, n=64):
         op("v", lambda: g.vector.tensor_copy(out, a), r, w, cyc(n))
 
-    def scan(out, a, b, r, w, n=64):
-        op("v", lambda: g.vector.tensor_tensor_scan(out, a, b, 0.0, A.mult, A.add), r, w, cyc(n))
+    def scan(out, a, b, init, r, w, n=64):
+        op("v", lambda: g.vector.tensor_tensor_scan(out, a, b, init, A.mult, A.add), r, w, cyc(n))
 
     def fill(out, v, w, n=64):
         op("v", lambda: g.vector.memset(out, v), [], w, cyc(n))
 
     def act(out, a, f, r, w, n=128, **kw):
-        op("a", lambda: g.scalar.activation(out, a, f, **kw), r, w, cyc(n) + 80)
+        op("a", lambda: g.scalar.activation(out, a, f, **kw), r, w, cyc(n) + 60)
 
     def iota(out, pat, base, cmul, key, n, **kw):
         op("g", lambda: g.iota(out, pat, base, cmul, **kw), [], [key], 160 + 2.1 * n)
@@ -157,259 +180,341 @@ def rank_program(g, core, T, topo):
     def col(buf, c):
         return buf[:, c:c + 1]
 
-    dma("s", T.cm[:, 0:96], T.came[:, 0:96], [], ["cm0"], "ld0", 16, 2100.0)
-    dma("s", T.cm[:, 288:384], T.came[:, 288:384], [], ["cm3"], "ld3", 16, 2200.0)
-    dma("s", T.cm[:, 96:288], T.came[:, 96:288], [], ["cm1", "cm2"], "ld1", 16, 2500.0)
+    raw = OPT["raw"]
+    r0 = raw[0] if raw else 4
+    dma("s", T.cm[:, 0:96], T.came[:, 0:96], [], ["cm0"], "ld0", 16, 2000.0)
+    if raw:
+        dma("s", T.cm[:, 96 * r0:96 * (raw[-1] + 1)], T.came[:, 96 * r0:96 * (raw[-1] + 1)], [], ["cm%d" % e for e in raw], "ld3", 16, 2200.0)
+    rest = [e for e in range(1, 4) if e not in raw]
+    dma("s", T.cm[:, 96 * rest[0]:96 * (rest[-1] + 1)], T.came[:, 96 * rest[0]:96 * (rest[-1] + 1)], [], ["cm%d" % e for e in rest], "ld1", 16, 2600.0)
     dma("a", T.hh[0:8, 0:27], T.hc[:], [], ["hh0"], "ld2", 32, 2100.0)
     dma("a", T.hh[0:8, 27:28], T.had[:], [], ["hh1"], "ld2", 32, 2100.0)
-    for k in range(4):
-        dma("s", T.W[:, 1024 * k:1024 * (k + 1)], T.ring[:, 1024 * k:1024 * (k + 1)], [], ["W%d" % k], "rg%d" % k, 16,
-            2500.0 + OPT["ring"] * (k + 1))
+    nr = OPT["ring"]
+    rw = P // nr
+    for k in range(nr):
+        dma("s", T.W[:, rw * k:rw * (k + 1)], T.ring[:, rw * k:rw * (k + 1)], [], ["W%d" % k], "rg%d" % k, 16,
+            2600.0 + OPT["load"] * (k + 1) / nr)
     nload = len(ops)
 
     small = {"allow_small_or_imprecise_dtypes": True}
     iota(T.pc[:, 0:1], [[0, 1]], 0, 1, "pc0", 1)
-    iota(T.iot[:, 384:512], [[16, 8], [0, 16]], 0, 0, "io3", 128, **small)
     iota(T.iot[:, 0:128], [[1, 128]], 0, 0, "io0", 128, **small)
-    iota(T.iot[:, 128:256], [[4, 32], [0, 4]], 0, 0, "io1", 128, **small)
+    iota(T.iot[:, 128:256], [[16, 8], [0, 16]], 0, 0, "io3", 128, **small)
     iota(T.iot[:, 256:384], [[16, 8], [0, 4], [1, 4]], 0, 0, "io2", 128, **small)
     fill(T.rst[:], 1.0, ["rst"], 144)
     fill(T.rst[:, 0:288:32], 0.0, ["rst"])
-    fill(mat(ZERO), 0.0, [mk(ZERO)])
+    fill(T.cb[:], 512.0, ["cb"], 144)
     fill(T.o8[0:8, :], 1.0, ["o8"], 128)
-    fill(col(tb, CUM), 0.0, ["cum0"])
     for c, m in ((1, 124), (2, 115), (3, 112)):
         ts(col(T.pc, c), col(T.pc, 0), m, None, A.bitwise_and, None, ["pc0"], ["pc%d" % c])
     cp(T.pf[:, 0:4], T.pc[:, 0:4], ["pc0", "pc1", "pc2", "pc3"], ["pf"])
-    ts(mat(ONES), T.iot[:, 384:512], col(T.pf, 3), None, A.is_equal, None, ["io3", "pf"], [mk(ONES)])
-    ts(mat(ID), T.iot[:, 0:128], col(T.pf, 0), None, A.is_equal, None, ["io0", "pf"], [mk(ID)])
-    ts(mat(TRI), T.iot[:, 0:128], col(T.pf, 0), -1.0, A.is_lt, A.mult, ["io0", "pf"], [mk(TRI)])
-    tt(mat(TRI), mat(TRI), mat(ONES), A.mult, [mk(TRI), mk(ONES)], [mk(TRI)], 128)
+    io0 = T.iot[:, 0:128]
+    ts(mat(ONES), T.iot[:, 128:256], col(T.pf, 3), None, A.is_equal, None, ["io3", "pf"], [mk(ONES)])
+    ts(mat(ID), io0, col(T.pf, 0), None, A.is_equal, None, ["io0", "pf"], [mk(ID)])
+    ts(T.i16[:], io0, col(T.pf, 0), None, A.is_equal, None, ["io0", "pf"], ["i16"])
+    ts(mat(TRI), io0, col(T.pf, 0), -1.0, A.is_lt, A.mult, ["io0", "pf"], [mk(TRI)])
+    tt(mat(TRI), mat(TRI), mat(ONES), A.mult, [mk(TRI), mk(ONES)], [mk(TRI)], 256)
     for a in range(4):
-        ts(mat(E1 + a), T.iot[:, 0:128], col(T.pf, 1), float(a), A.subtract, A.is_equal, ["io0", "pf"], [mk(E1 + a)])
-        ts(mat(E2 + a), T.iot[:, 0:128], col(T.pf, 2), float(4 * a), A.subtract, A.is_equal, ["io0", "pf"], [mk(E2 + a)])
-    ts(mat(B1), T.iot[:, 128:256], col(T.pf, 1), 0.25, A.is_equal, A.mult, ["io1", "pf"], [mk(B1)])
+        ts(mat(E1 + a), io0, col(T.pf, 1), float(a), A.subtract, A.is_equal, ["io0", "pf"], [mk(E1 + a)])
+        ts(mat(E2 + a), io0, col(T.pf, 2), float(4 * a), A.subtract, A.is_equal, ["io0", "pf"], [mk(E2 + a)])
     ts(mat(B2), T.iot[:, 256:384], col(T.pf, 2), 0.25, A.is_equal, A.mult, ["io2", "pf"], [mk(B2)])
-    iota(T.crow[:], [[512, 4], [0, 72]], 512, 0, "crow", 288, **small)
+    nbm = 3 * max(len(b) for b in OPT["batches"] + [raw])
+    iota(T.crow[:, 0:16 * nbm], [[512, 4], [0, 4 * nbm]], 512, 0, "crow", 16 * nbm, **small)
     op("g", lambda: g.affine_select(T.e8[0:8, :], T.o8[0:8, :], [[1, 8], [0, 16]], A.is_equal, 0.0, 0, -1), ["o8"], ["e8"], 480.0)
-    iota(T.ps[:, FO:FO + 256], [[16, 256]], -2047, 1, "ps4", 256)
-    for i, sc in ((ID4, 0.25), (IDN, -1.0), (BIG, 8192.0)):
+    for i, sc in ((ID4, 0.25), (IDN, -1.0)):
         act(mat(i), mat(ID), AF.Copy, [mk(ID)], [mk(i)], scale=sc)
-    act(T.m32[:, 0:128], mat(ID), AF.Copy, [mk(ID)], ["i32"])
+    act(T.i32[:], mat(ID), AF.Copy, [mk(ID)], ["i32"])
 
     def flags(src, lo, n, r, key):
         cp(T.F[:, lo:lo + n], src, r, ["F" + key], n)
-        scan(T.S[:, lo:lo + n], T.rst[:, 0:n], T.F[:, lo:lo + n], ["rst", "F" + key], ["S" + key], n // 2)
+        scan(T.S[:, lo:lo + n], T.rst[:, 0:n], T.F[:, lo:lo + n], 0.0, ["rst", "F" + key], ["S" + key], n // 2)
 
-    def lists(lo, nb, key, b0, b1):
+    def lists(lo, nb, key, b0, b1, b2):
         n = 32 * nb
-        Bb, Rb = T.Bb[:, lo:lo + n], T.Rb[:, lo:lo + n]
+        bl, dup = 2 * lo, OPT["dup"][key]
+        Bb, Rb = T.Bb[:, bl:bl + n], T.Rb[:, lo:lo + n]
         pl = 4 * lo
         kb, kr = "Bb" + key, "Rb" + key
         kp = ["Ps%s_%d" % (key, a) for a in range(4)]
         ps = lambda a: T.Ps[:, pl + a * n:pl + (a + 1) * n]
+        X = lambda b: T[b][:, 0:n]
 
         def split(bank, h):
             m = 1.5 * 2 ** 23 * 4 * h
-            V = T[bank][:, 0:n]
-            ts(Bb, V, m, m, A.add, A.subtract, [bank], [kb], n)
-            tt(Rb, V, Bb, A.subtract, [bank, kb], [kr], n)
+            ts(Bb, X(bank), m, m, A.add, A.subtract, [bank], [kb], n)
+            if h == 16 and dup == 2:
+                ts(T.Bb[:, bl + n:bl + 2 * n], X(bank), m, m, A.add, A.subtract, [bank], [kb + "'"], n)
+            tt(Rb, X(bank), Bb, A.subtract, [bank, kb], [kr], n)
             h = float(h)
-            for a, (s1, s2, o0, o1) in enumerate(((0.0, h, A.max, A.min), (-h, 0.0, A.add, A.max),
-                                                  (h, 0.0, A.add, A.min), (-h, 0.0, A.max, A.min))):
+            act(ps(1), Rb, AF.Relu, [kr], [kp[1]], n, bias=-h)
+            for a, s1, s2, o0, o1 in ((0, 0.0, h, A.max, A.min), (2, h, 0.0, A.add, A.min), (3, -h, 0.0, A.max, A.min)):
                 ts(ps(a), Rb, s1, s2, o0, o1, [kr], [kp[a]], n // 2)
 
-        mms(b0, [(T[b0][:, 0:n], mat(TRI), T.F[:, lo:lo + n], ["F" + key, mk(TRI)], n),
-                 (T[b0][:, 0:n], mat(ONES), T.S[:, lo:lo + n], ["S" + key, mk(ONES)], n)])
-        for src, dst, h, eb, bb in ((b0, b1, 1, E1, B1), (b1, b0, 4, E2, B2)):
-            split(src, h)
-            mms(dst, [(T[dst][:, 0:n], mat(bb), Bb, [kb, mk(bb)], n)] +
-                [(T[dst][:, 0:n], mat(eb + a), ps(a), [kp[a], mk(eb + a)], n) for a in range(4)])
+        l1 = OPT["l1"][key]
+        if l1 == 4:
+            b2 = b0
+        for b in sorted({b0, b2}):
+            mms(b, [(X(b), mat(TRI), T.F[:, lo:lo + n], ["F" + key, mk(TRI)], n),
+                    (X(b), mat(ONES), T.S[:, lo:lo + n], ["S" + key, mk(ONES)], n)])
+        for a in range(4):
+            if a < 4 - l1:
+                ts(ps(a), X(b0), 0.25, 128 + (1.5 - a) / 4, A.mult, A.add, [b0], [kp[a]], n)
+            else:
+                act(ps(a), X(b2), AF.Identity, [b2], [kp[a]], n, scale=0.25, bias=128 + (1.5 - a) / 4)
+        mms(b1, [(X(b1), mat(E1 + a), ps(a), [kp[a], mk(E1 + a)], n) for a in (0, 2, 1, 3)])
+        split(b1, 4)
+        mms(b0, [(X(b0), mat(B2), Bb, [kb, mk(B2)], n)] + [(X(b0), mat(E2 + a), ps(a), [kp[a], mk(E2 + a)], n) for a in (0, 2, 1, 3)])
         split(b0, 16)
         k = n // 4
-        mms(b1, [(T[b1][:, 0:n], mat(ZERO), Bb, [kb, mk(ZERO)], n)] +
-            [(T[b1][:, a * k:(a + 1) * k], mat(ID4), T.Bb[:, lo + c:lo + n:4], [kb, mk(ID4)], k) for a in range(4) for c in range(4)] +
-            [(T[b1][:, 0:n], mat(ID), T.Ps[:, pl + c:pl + 4 * n:4], kp + [mk(ID)], n) for c in range(4)])
+        mms(b1, [(X(b1), mat(IDN), T.cb[:, 0:n], ["cb", mk(IDN)], n)] +
+            [(T[b1][:, a * k:(a + dup) * k], mat(ID4), T.Bb[:, bl + c:bl + dup * n:4], [kb, kb + "'", mk(ID4)], dup * k)
+             for a in range(0, 4, dup) for c in range(4)] +
+            [(X(b1), mat(ID), T.Ps[:, pl + c:pl + 4 * n:4], kp + [mk(ID)], n) for c in range(4)])
         if nb > 3:
-            cp(Rb, T[b1][:, 0:n], [b1], [kr], n)
+            act(Rb, X(b1), AF.Copy, [b1], [kr], n)
         for a in range(4):
             if nb > 3:
                 ts(ps(a), Rb, 64.0 * a, 64.0 * a + 64.0, A.max, A.min, [kr], [kp[a]], n // 2)
             else:
-                ts(ps(a), T[b1][:, 0:n], 64.0 * a, 64.0 * a + 64.0, A.max, A.min, [b1], [kp[a]], n)
+                ts(ps(a), X(b1), 64.0 * a, 64.0 * a + 64.0, A.max, A.min, [b1], [kp[a]], n)
         w = 16 * nb
-        mms(b0, [(T[b0][:, 0:w], mat(ID), T.crow[:, 0:288:18 // nb], ["crow", mk(ID)], w)] +
+        mms(b0, [(T[b0][:, 0:w], mat(ID), T.crow[:, 0:16 * nbm:nbm // nb], ["crow", mk(ID)], w)] +
             [(T[b0][:, 0:w], mat(IDN), T.Ps[:, pl + c:pl + 4 * n:8], kp + [mk(IDN)], w) for c in range(8)])
 
     sent = [0]
     order = dest_order(cores, rank, topo)
-    masks = split_masks(topo.engines(core, cores[(rank + 1) % N]))
+    engines = topo.engines(core, cores[(rank + 1) % N])
+    masks = split_masks(engines)
     nmask = sum(m[1] for m in masks)
+    peer = lambda d: DstId(rid=topo.addr(cores[(rank + d) % N])[0], pnc=topo.addr(cores[(rank + d) % N])[1])
+
+    def send(trs, name, r, w, after, n_out, n_in):
+        op("g", lambda: g.remote_dma_fused(trs, local_sem=sem.sent), r, ["x" + name, "gl"], 300.0, 0.0, ("", 0))
+        sent[0] += n_out
+        op("x", None, ["x" + name], w, 0.0, after, (name, n_in))
 
     def to_makers(src, dst, name, r, w, after):
-        trs = []
-        for d in range(1, N):
-            q = (rank + d) % N
-            rid, pid, _ = topo.addr(cores[q])
-            pos = dest_order(cores, q, topo).index(rank)
-            trs.append(RemoteDMATransfer(dst_ids=[DstId(rid=rid, pnc=pid)], dma_engine_mask=masks[d - 1][0], remote_sem=sem[name],
-                                         src=src(d - 1), dst=dst(pos)))
-        op("g", lambda: g.remote_dma_fused(trs, local_sem=sem.sent), r, ["x" + name, "gq"], 300.0, 0.0, ("", 0))
-        sent[0] += nmask
-        op("x", None, ["x" + name], w, 0.0, after, (name, nmask))
+        send([RemoteDMATransfer(dst_ids=[peer(d)], dma_engine_mask=masks[d - 1][0], remote_sem=sem[name], src=src(d - 1), dst=dst(3 - d))
+              for d in range(1, N)], name, r, w, after, nmask, nmask)
 
     xs = {}
-    to_makers(lambda d: T.cm[:, 288 + 32 * d:320 + 32 * d], lambda p: T.fl[:, 32 * p:32 * p + 32], "afl", ["cm3"], ["fl"],
-              OPT["lats"] + OPT["first"])
-    banks = [("pL", "pM"), ("pD", "pC"), ("pL", "pM")]
-    for i, rounds in enumerate(OPT["batches"]):
+    banks = [("pL", "pM", "pD"), ("pT", "pF", "pC"), ("pL", "pM", "pC")]
+    first = OPT["first"]
+    if raw:
+        for e in raw:
+            to_makers(lambda d: T.cm[:, 96 * e + 32 * d:96 * e + 32 * d + 32], lambda p: T.fl[:, 96 * (e - r0) + 32 * p:96 * (e - r0) + 32 * p + 32],
+                      "afl", ["cm%d" % e], ["fl"], OPT["lats"] + first)
+        ops[-1]["tok"] = ("afl", nmask * len(raw))
+        first = 0.0
+    for rounds in OPT["batches"]:
+        e0, ne = rounds[0], len(rounds)
+        flags(T.cm[:, 96 * e0:96 * (e0 + ne)], 96 * e0, 96 * ne, ["cm%d" % e for e in rounds], str(e0))
+
+    def batch(i, first):
+        rounds = OPT["batches"][i]
         e0, ne = rounds[0], len(rounds)
         key = str(e0)
-        flags(T.cm[:, 96 * e0:96 * (e0 + ne)], 96 * e0, 96 * ne, ["cm%d" % e for e in rounds], key)
+        lo_i = 152 * e0
         lists(96 * e0, 3 * ne, key, *banks[i])
-        k, o = 16 * ne, 48 * e0
-        for d in range(3):
-            ts(T.Lo[:, o + d * k:o + (d + 1) * k], T[banks[i][0]][:, d:3 * k:3], 512.0 * rank, None, A.add, None, [banks[i][0]], ["Lo%s_%d" % (key, d)])
-        to_makers(lambda d, o=o, k=k: T.Lo[:, o + d * k:o + (d + 1) * k], lambda p, o=o, k=k: T.Li[:, o + p * k:o + (p + 1) * k],
-                  "al%d" % i, ["Lo%s_%d" % (key, d) for d in range(3)], ["Li" + key], OPT["lats"])
-        for e in rounds:
-            xs[e] = (T.Li[:, o + e - e0:o + 3 * k:ne], ["Li" + key])
-    flags(T.cm[:, 288:384], 288, 96, ["cm3"], "3")
-    flags(T.fl[:], 384, 96, ["fl"], "4")
-    lists(384, 3, "4", "pL", "pM")
-    for p in range(3):
-        ts(T.L3[:, 16 * p:16 * p + 16], T.pL[:, p:48:3], 512.0 * order[p], None, A.add, None, ["pL"], ["L3_%d" % p])
-    xs[3] = (T.L3[:], ["L3_0", "L3_1", "L3_2"])
+        k, o, b = 16 * ne, 48 * e0, banks[i][0]
+        if OPT["multi"]:
+            ts(T.Lo[:, o:o + 3 * k], T[b][:, 0:3 * k], 512.0 * rank, None, A.add, None, [b], ["Lo" + key], 3 * k)
+            tr = RemoteDMATransfer(dst_ids=[peer(d) for d in range(1, N)], dma_engine_mask=sum(1 << e for e in engines), remote_sem=sem["al%d" % i],
+                                   srcs=[T.Lo[:, o:o + 3 * k]],
+                                   dsts=[T.Li[:, lo_i + (3 - d) * (3 * k + 1):lo_i + (3 - d) * (3 * k + 1) + 3 * k] for d in range(1, N)])
+            send([tr], "al%d" % i, ["Lo" + key], ["Li" + key], OPT["lats"] + first, len(engines), 3 * len(engines))
+            for e in rounds:
+                xs[e] = (T.Li[:, lo_i + 2 + 3 * (e - e0):lo_i + 9 * k + 2:3 * ne], ["Li" + key])
+        else:
+            for d in range(3):
+                ts(T.Lo[:, o + d * k:o + (d + 1) * k], T[b][:, d:3 * k:3], 512.0 * rank, None, A.add, None, [b], ["Lo%s_%d" % (key, d)])
+            to_makers(lambda d: T.Lo[:, o + d * k:o + (d + 1) * k], lambda p: T.Li[:, o + p * k:o + (p + 1) * k],
+                      "al%d" % i, ["Lo%s_%d" % (key, d) for d in range(3)], ["Li" + key], OPT["lats"] + first)
+            for e in rounds:
+                xs[e] = (T.Li[:, o + e - e0:o + 3 * k:ne], ["Li" + key])
 
-    for k in range(4):
-        sl = T.W[:, 1024 * k:1024 * (k + 1)]
-        act(sl, sl, AF.Copy, ["W%d" % k], ["W%d" % k], 1024, scale=1.0 / 256)
+    op("g", lambda: g.iota(T.j0[:], [[16, 256]], -2047, 1, **small), ["gl"], ["j0"], 700.0)
+    batch(0, first)
+    skeys = ["S%d" % b[0] for b in OPT["batches"]]
+    if raw:
+        flags(T.cm[:, 96 * r0:96 * (raw[-1] + 1)], 96 * r0, 96 * len(raw), ["cm%d" % e for e in raw], "r")
+        skeys.append("Sr")
+    mms("pB", [(T.pB[:, 0:12], mat(ONES), T.S[:, 31:384:32], skeys + [mk(ONES)], 64)])
+
+    for k, eng in enumerate(OPT["scale"]):
+        sl, key = T.W[:, 512 * k:512 * (k + 1)], "W%d" % (k * nr // 8)
+        if eng == "a":
+            act(sl, sl, AF.Copy, [key], ["V%d" % k], 512, scale=1.0 / 256)
+        else:
+            ts(sl, sl, 1.0 / 256, None, A.mult, None, [key], ["V%d" % k], 256)
 
     ts(T.hh[0:8, 28:29], T.hh[0:8, 27:28], 4095, None, A.bitwise_and, None, ["hh0", "hh1"], ["hh2"])
     cp(T.hf[0:8, 0:29], T.hh[0:8, 0:29], ["hh0", "hh1", "hh2"], ["hf"])
-    mms("pT", [(T.pT[:, 0:29], T.e8[0:8, :], T.hf[0:8, 0:29], ["e8", "hf"], 256)])
-    cp(T.C[:, 0:29], T.pT[:, 0:29], ["pT"], ["C"])
-    mms("pF", [(T.pF[:, 0:12], mat(ONES), T.S[:, 31:384:32], ["S%d" % b[0] for b in OPT["batches"]] + ["S3", mk(ONES)], 64)])
+    mms("pA", [(T.pA[:, 0:29], T.e8[0:8, :], T.hf[0:8, 0:29], ["e8", "hf"], 256)])
+    act(T.C[:, 0:29], T.pA[:, 0:29], AF.Copy, ["pA"], ["C"], 64)
     for k in range(3):
         act(mat(FD + k), mat(ID), AF.Copy, [mk(ID), "C"], [mk(FD + k)], scale=col(T.C, 24 + k))
     had, h0 = col(T.C, 27), col(T.C, 28)
     t12 = lambda c: tb[:, c:c + 12]
-    t13 = lambda c: tb[:, c:c + 13]
     t4 = lambda c: tb[:, c:c + 4]
+    cnts, one = T.pB[:, 0:12], T.rst[:, 1:13]
     ts(col(tb, CC), had, 4096.0, 1.0 / 4096, A.min, A.mult, ["C"], ["cc0"])
-    scan(t12(CUM + 1), T.rst[:, 1:13], T.pF[:, 0:12], ["rst", "pF"], ["cum"])
-    ts(t12(GN), T.pF[:, 0:12], -256.0, None, A.add, None, ["pF"], ["gn"])
-    ts(t12(GH), T.pF[:, 0:12], -256.0, 0.5, A.add, A.mult, ["pF"], ["gh"])
-    ts(t4(MM), tb[:, CUM + 3:CUM + 13:3], had, None, A.add, None, ["cum", "C"], ["mm"])
-    ts(t4(CC + 1), t4(MM), 4096.0, 1.0 / 4096, A.min, A.mult, ["mm"], ["cc1"])
-    dma("s", T.now[:], tb[0:128:16, MM + 3:MM + 4], ["mm"], ["now"], "stn", 16, 2000.0)
-    ts(t13(TH), t13(CUM), h0, None, A.add, None, ["cum0", "cum", "C"], ["th"])
-    ts(t13(NW), t13(TH), 4096.0, None, A.is_lt, None, ["th"], ["nw"])
-    ts(t13(GW), t13(TH), 4096.0, -4096.0, A.is_ge, A.mult, ["th"], ["gw"])
-    tt(t13(TH), t13(TH), t13(GW), A.add, ["th", "gw"], ["th"])
-    tt(t12(GW), t12(GN), t12(NW + 1), A.mult, ["gn", "nw"], ["gw"])
-    scan(t12(SG), T.rst[:, 1:13], t12(GW), ["rst", "gw"], ["sg"])
-    scan(t12(SH), T.rst[:, 1:13], t12(GH), ["rst", "gh"], ["sh"])
-    ts(col(tb, HC), h0, -1.0, 6144.0, A.mult, A.add, ["C"], ["hc"])
-    ts(t4(CON), tb[:, NW + 3:NW + 13:3], -16384.0, col(tb, HC), A.mult, A.add, ["nw", "hc"], ["con"])
-    tt(t4(CON), t4(CON), tb[:, SG + 1:SG + 12:3], A.subtract, ["con", "sg"], ["con"])
-    ts(t4(WH), tb[:, SH + 1:SH + 12:3], -1.0, -6144.0, A.mult, A.add, ["sh"], ["wh"])
-    for e in range(1, 5):
-        o = THR + 16 * (e - 1)
-        ts(tb[:, o:o + 3 * e + 1], tb[:, TH:TH + 3 * e + 1], col(tb, CON + e - 1), -2047.5, A.add, A.add, ["th", "con"], ["thr%d" % e])
-        act(T.m32[:, 128 * e:128 * (e + 1)], mat(ID), AF.Copy, [mk(ID), "wh"], ["w32%d" % e], scale=col(tb, WH + e - 1))
-    for b in range(11):
-        act(mat(GD + b), mat(ID), AF.Copy, [mk(ID), "gn", "gh"], [mk(GD + b)], scale=col(tb, (GN if b in OPT["vset"] else GH) + b))
+    act(col(tb, H2), h0, AF.Identity, ["C"], ["h2"], 64, bias=-2047.0)
+    act(col(tb, NW), h0, AF.Identity, ["C"], ["nw"], 64, bias=-4096.0)
+    scan(t12(THR), one, cnts, col(tb, H2), ["rst", "pB", "h2"], ["thr"])
+    scan(t12(MR), one, cnts, had, ["rst", "pB", "C"], ["mr"])
+    ts(t12(NG), cnts, -256.0, None, A.add, None, ["pB"], ["ng"])
+    for i in range(1, len(OPT["batches"])):
+        batch(i, 0.0)
+    ts(tb[:, CC + 1:CC + 4], tb[:, MR + 2:MR + 9:3], 4096.0, 1.0 / 4096, A.min, A.mult, ["mr"], ["cc1"])
+    dma("s", T.now[:], tb[0:128:16, MR + 11:MR + 12], ["mr"], ["now"], "stn", 16, 2000.0)
+    ts(t12(WR), t12(THR), 4096.0 - 2047.0, 4096.0, A.is_ge, A.mult, ["thr"], ["wr"])
+    tt(t12(TH), t12(THR), t12(WR), A.subtract, ["thr", "wr"], ["th"])
+    scan(t12(SH), one, t12(NG), col(tb, NW), ["rst", "ng", "nw"], ["sh"])
+    tt(t4(WE), tb[:, WR + 2:WR + 12:3], tb[:, SH + 1:SH + 12:3], A.subtract, ["wr", "sh"], ["we"])
+    tt(t12(XU), t12(NG), t12(WR), A.add, ["ng", "wr"], ["xu"])
+    ts(t12(XU), t12(XU), 0.0, None, A.min, None, ["xu"], ["xu"])
+    scan(t12(ZU), one, t12(XU), col(tb, NW), ["rst", "xu", "nw"], ["zu"])
+    ts(t4(KK), tb[:, WR + 2:WR + 12:3], col(tb, ZU + 11), -1.0 / 4096, A.mult, A.mult, ["wr", "zu"], ["kk"])
+    if OPT["signs"]:
+        act(mat(HALF), mat(ID), AF.Copy, [mk(ID)], [mk(HALF)], scale=0.5)
+        act(col(tb, ZC), col(tb, ZU + 11), AF.Identity, ["zu"], ["zc"], 64, scale=-1.0 / 4096, bias=0.5)
+        act(t4(KS), tb[:, WR + 2:WR + 12:3], AF.Copy, ["wr", "zc"], ["ks"], 64, scale=col(tb, ZC))
+        act(T.m32[:, 0:128], mat(HALF), AF.Copy, [mk(HALF), "nw"], ["w0"], scale=col(tb, NW))
+        for e in OPT["signs"]:
+            act(T.m32[:, 128 * e:128 * (e + 1)], mat(HALF), AF.Copy, [mk(HALF), "we"], ["w%d" % e], scale=col(tb, WE + e - 1))
+        for b in range(3 * max(OPT["signs"]) - 1):
+            act(mat(GD + b), mat(HALF), AF.Copy, [mk(HALF), "ng"], [mk(GD + b)], scale=col(tb, NG + b))
+
+    if raw:
+        ne = len(raw)
+        flags(T.fl[:, 0:96 * ne], 384, 96 * ne, ["fl"], "4")
+        lists(384, 3 * ne, "4", *banks[2])
+        k = 16 * ne
+        for p in range(3):
+            ts(T.L3[:, k * p:k * p + k], T.pL[:, p:3 * k:3], 512.0 * ((rank - 3 + p) % N), None, A.add, None, ["pL"], ["L3_%d" % p])
+        for e in raw:
+            xs[e] = (T.L3[:, e - r0:3 * k:ne], ["L3_0", "L3_1", "L3_2"])
 
     def places(e):
         x, xk = xs[e]
-        o = e * HW
-        zs = ["z%d_%d" % (e, k) for k in range(3)]
-        z, u, s = T.z[:, o:o + HW], T.u[:, o:o + HW], T.s[:, o:o + HW]
-        ku, ks = "u%d" % e, "s%d" % e
-        for k in range(3):
-            ts(T.z[:, o + 48 * k:o + 48 * (k + 1)], x, col(T.C, 6 * e + k), col(T.C, 6 * e + 3 + k), A.mult, A.add, xk + ["C"], [zs[k]])
-        ts(u, z, 4095, None, A.bitwise_and, None, zs, [ku], HW)
-        ts(s, u, 2.0, -4095.0, A.mult, A.add, [ku], [ks], HW)
-        tt(z, u, s, A.mult, [ku, ks], zs, 2 * HW)
-        ts(u, z, 4095, None, A.bitwise_and, None, zs, [ku], HW)
-        if e == 0:
-            ts(T.pp[:, 0:HW], u, col(tb, CC), -2047.5 + 2.0 ** -13, A.mult, A.add, [ku, "cc0"], ["pp0"], HW)
-            ts(T.off[:, 0:HW], T.pp[:, 0:HW], 2047.0, None, A.add, None, ["pp0"], ["off0"], HW)
-        else:
-            ts(T.pp[:, o:o + HW], u, col(tb, CC + e), -2047.5 + 2.0 ** -13, A.mult, A.add, [ku, "cc1"], ["pp%d" % e], HW)
+        for ks in ([[2], [0], [1]] if e < OPT["hsplit"] else [[0, 1, 2]]):
+            o, n = e * HW + 48 * ks[0], 48 * len(ks)
+            name = lambda s: ["%s%d_%d" % (s, e, k) for k in ks]
+            z, u, s, pp = T.z[:, o:o + n], T.u[:, o:o + n], T.pD[:, 0:n], T.pp[:, o:o + n]
+            for k in ks:
+                c = e * HW + 48 * k
+                ts(T.z[:, c:c + 48], x, col(T.C, 6 * e + k), col(T.C, 6 * e + 3 + k), A.mult, A.add, xk + ["C"], ["z%d_%d" % (e, k)])
+            ts(u, z, 4095, None, A.bitwise_and, None, name("z"), name("u"), n)
+            if len(ks) == 1:
+                ts(pp, u, 2.0, -4095.0, A.mult, A.add, name("u"), name("pp"), n)
+                tt(z, u, pp, A.mult, name("u") + name("pp"), name("z"), 2 * n)
+            else:
+                ts(s, u, 2.0, -4095.0, A.mult, A.add, name("u"), ["pD"], n)
+                tt(z, u, s, A.mult, name("u") + ["pD"], name("z"), n)
+            ts(u, z, 4095, None, A.bitwise_and, None, name("z"), name("u"), n)
+            ts(pp, u, col(tb, CC + e), -2047.5 + 2.0 ** -13, A.mult, A.add, name("u") + ["cc1" if e else "cc0"], name("pp"), n)
+            if e == 0:
+                ts(T.off[:, o:o + n], pp, 2047.0, None, A.add, None, name("pp"), name("off"), n)
+            elif e in OPT["signs"]:
+                ts(T.jf[:, o:o + n], pp, 0.5, None, A.add, None, name("pp"), ["jh%d" % e], n)
+            else:
+                cp(T.jh[:, o:o + n], pp, name("pp"), ["jh%d" % e], n)
+        if e:
             positions(e)
 
     def positions(e):
-        o, n, bank = (e * HW, HW, "pT") if e < 4 else (FO, 256, "pF")
-        pp, jf, kp, kj = T.pp[:, o:o + n], T.jf[:, o:o + n], "pp%d" % e, "jf%d" % e
-        nb, th, kt = 3 * e, THR + 16 * (e - 1), "thr%d" % e
+        o, n, bank = (e * HW, HW, "pL" if e in raw else "pT") if e < 4 else (FO, 256, "pF")
+        jh, kj = T.jh[:, o:o + n], "jh%d" % e
         so = HW * (3 * e * (e - 1) // 2)
-        ts(jf, pp, col(tb, CON + e - 1), None, A.add, None, [kp, "con"], [kj], n)
-        act(T.sh[:, o:o + n], jf, AF.Sign, [kj, kt], ["sh%d" % e], n, bias=col(tb, th), scale=-1.0)
         X = T[bank][:, 0:n]
-        items = [(X, T.m32[:, 0:128], jf, ["i32", kj], 4 * n),
-                 (X, T.m32[:, 128 * e:128 * (e + 1)], T.sh[:, o:o + n], ["w32%d" % e, "sh%d" % e], 4 * n)]
-        for b in range(nb):
-            sl, k = T.sg[:, so + b * n:so + (b + 1) * n], "sg%d_%d" % (e, b)
-            if b in OPT["vset"] and b < nb - 1:
-                ts(sl, jf, col(tb, th + 1 + b), -0.5, A.is_lt, A.add, [kj, kt], [k], n)
+        if e in OPT["signs"]:
+            jf = T.jf[:, o:o + n]
+            items = [(X, T.i32[:], jf, ["i32", kj], 4 * n)]
+            for b in [0, 3 * e] + list(range(1, 3 * e)):
+                k, c = "sg%d_%d" % (e, b), o + (FO + 256) * (b > 0)
+                sl = T.big[:, c:c + n] if b in (0, 3 * e) else T.sg[:, so + b * n:so + (b + 1) * n]
+                act(sl, jf, AF.Sign, [kj, "th", "h2"], [k], n, bias=col(tb, TH + b - 1) if b else col(tb, H2), scale=-1.0)
+                if b in (0, 3 * e):
+                    i = e if b else 0
+                    items.append((X, T.m32[:, 128 * i:128 * (i + 1)], sl, [k, "w%d" % i], 4 * n))
+                else:
+                    items.append((X, mat(GD + b - 1), sl, [k, mk(GD + b - 1)], n))
+            mms(bank, items)
+            ts(T.off[:, o:o + n], X, col(tb, KS + e - 1), 2046.5, A.add, A.add, [bank, "ks"], ["off%d_%d" % (e, k) for k in range(3)], n)
+            return
+        items = [(X, T.i16[:], jh, ["i16", kj], n)]
+        for b in [0, 3 * e] + list(range(1, 3 * e)):
+            k = "sg%d_%d" % (e, b)
+            th = col(tb, TH + b - 1) if b else col(tb, H2)
+            if b in (0, 3 * e):
+                c = o + (FO + 256) * (b > 0)
+                ts(T.big[:, c:c + n], jh, th, col(tb, WE + e - 1) if b else col(tb, NW), A.is_lt, A.mult, [kj, "th", "h2", "nw", "we"], [k], n)
+                items.append((X, T.i32[:], T.big[:, c:c + n], [k, "i32"], 4 * n))
             else:
-                act(sl, jf, AF.Sign, [kj, kt], [k], n, bias=col(tb, th + 1 + b), scale=-1.0)
-            m = BIG if b == nb - 1 else GD + b
-            items.append((X, mat(m), sl, [k, mk(m)], n))
+                sl = T.sg[:, so + b * n:so + (b + 1) * n]
+                ts(sl, jh, th, col(tb, NG + b - 1), A.is_lt, A.mult, [kj, "th", "ng"], [k], n // 2)
+                items.append((X, mat(ID), sl, [k, mk(ID)], n))
         mms(bank, items)
-        tt(T.ps[:, o:o + n], X, pp, A.max, [bank, kp], ["ps%d" % e], n)
-        ts(T.off[:, o:o + n], T.ps[:, o:o + n], 2047.0, None, A.add, None, ["ps%d" % e], ["off%d" % e], n)
+        ts(T.off[:, o:o + n], X, col(tb, KK + e - 1), 2047.0, A.add, A.add, [bank, "kk"], ["off%d_%d" % (e, k) for k in range(3)], n)
 
     def window(e):
-        return T.W[:, 0:P + 3 * CAP * e], ["W0", "W1", "W2", "W3"] + ["land%d" % i for i in range(e)]
+        return T.W[:, 0:P + 3 * CAP * e], ["V%d" % k for k in range(8)] + ["land%d_%d" % (i, j) for i in range(e) for j in range(3)]
+
+    def gather(eng, dst, src, r, w, n, scale=None):
+        c = (1.56 * n + 50) * 1.04
+        if eng == "a":
+            op("a", lambda: g.scalar.activation(dst, src, AF.Copy, scale=scale or 1.0), r, w, c + 15)
+        elif scale:
+            op("v", lambda: g.vector.tensor_scalar(dst, src, scale, None, A.mult), r, w, c)
+        else:
+            op("v", lambda: g.vector.tensor_copy(dst, src), r, w, c)
 
     def make(e):
         win, wk = window(e)
         for j in range(3):
-            bank = "p" + "ABC"[j]
-            x, qq, o = T[bank][:, 0:CAP], T.q[:, j * CAP:(j + 1) * CAP], T.out[:, (3 * e + j) * CAP:(3 * e + j + 1) * CAP]
-            items = []
-            for k in (2, 0, 1):
-                c = e * HW + 48 * k + 16 * j
-                src = win.indirect(T.off[:, c:c + 16])
-                dst, key = T.G[:, (3 * j + k) * CAP:(3 * j + k + 1) * CAP], "G%d_%d" % (j, k)
-                if k < 2:
-                    act(dst, src, AF.Copy, wk + ["off%d" % e], [key], 1.56 * CAP)
-                else:
-                    cp(dst, src, wk + ["off%d" % e], [key], 1.56 * CAP + 60)
-                items.append((x, mat(FD + k), dst, [key, mk(FD + k)], CAP))
-            mms(bank, items)
-            ts(qq, x, -127.5 / 256, None, A.add, None, [bank], ["q%d" % j], CAP)
-            tt(o, x, qq, A.subtract, [bank, "q%d" % j], ["o%d" % (3 * e + j)], CAP)
             r = order[j]
+            piece = 3 - (rank - r) % N
+            oo, a, done = (3 * e + j) * CAP, 0, []
+            for i, n in enumerate(OPT["cuts"][j]):
+                bank = ("pA", "pB", "pC")[j] if i == 0 else "pA"
+                x, qq = T[bank][:, 0:n], T.q[:, j * CAP + a:j * CAP + a + n]
+                items = []
+                for k in (2, 0, 1):
+                    c = e * HW + 48 * k + 16 * piece + a // 16
+                    go, key = (3 * j + k) * CAP + a, "G%d_%d_%d" % (j, k, i)
+                    gather("v" if (j, k, i) in OPT["vg"] else "a", T.G[:, go:go + n], win.indirect(T.off[:, c:c + n // 16]),
+                           wk + ["off%d_%d" % (e, k)], [key], n)
+                    items.append((x, mat(FD + k), T.G[:, go:go + n], [key, mk(FD + k)], n))
+                mms(bank, items)
+                done.append("o%d_%d" % (3 * e + j, i))
+                ts(qq, x, -127.5 / 256, None, A.add, None, [bank], ["q%d_%d" % (j, i)], n)
+                tt(T.out[:, oo + a:oo + a + n], x, qq, A.subtract, [bank, "q%d_%d" % (j, i)], done[-1:], n)
+                a += n
+            o = T.out[:, oo:oo + CAP]
             rid, pid, _ = topo.addr(cores[r])
             c = P + (3 * e + (rank - r) % N - 1) * CAP
             op("g", lambda c=c, o=o, r=r, pid=pid, rid=rid: g.remote_dma(T.W[:, c:c + CAP], o, sem["ar%d" % e], sem.sent, pid, rid,
                                                                          topo.mask(core, cores[r])),
-               ["o%d" % (3 * e + j)], ["x%d_%d" % (e, j), "gq"], 300.0, OPT["gap"] * (2 - j), ("", 0))
+               done, ["x%d_%d" % (e, j), "gq"], 300.0, 0.0, ("", 0))
             sent[0] += len(topo.engines(core, cores[r]))
-        op("x", None, ["x%d_%d" % (e, j) for j in range(3)], ["land%d" % e], 0.0, OPT["lat"],
-           ("ar%d" % e, sum(len(topo.engines(cores[q], core)) for q in range(N) if q != rank)))
+            op("x", None, ["x%d_%d" % (e, j)], ["land%d_%d" % (e, j)], 0.0, OPT["lat"] + OPT["gap"] * (2 - j),
+               ("ar%d" % e, sum(len(topo.engines(cores[q], core)) for q in range(N) if q != rank)))
 
     for e in range(4):
         places(e)
         make(e)
-    ts(T.pp[:, FO:FO + 256], T.ps[:, FO:FO + 256], col(T.pf, 3), None, A.subtract, None, ["ps4", "pf"], ["pp4"], 256)
+    ts(T.jh[:, FO:FO + 256], T.j0[:], col(T.pf, 3), None, A.subtract, None, ["j0", "pf"], ["jh4"], 256)
     positions(4)
 
     win, wk = window(4)
     c = 0
     for i, n in enumerate(OPT["chunks"]):
-        src = win.indirect(T.off[:, FO + c // 16:FO + (c + n) // 16])
-        dst = T.Y[:, c:c + n]
-        if i % 2:
-            act(dst, src, AF.Copy, wk + ["off4"], ["Y%d" % i], 1.56 * n, scale=256.0)
-        else:
-            ts(dst, src, 256.0, None, A.mult, None, wk + ["off4"], ["Y%d" % i], 1.56 * n)
-        dma("s", T.y[:, c:c + n], dst, ["Y%d" % i], ["yq"], "st", 0, 3.0 * n)
-        c += n
+        for h, eng in enumerate("va"):
+            a = c + h * n
+            gather(eng, T.Y[:, a:a + n], win.indirect(T.off[:, FO + a // 16:FO + (a + n) // 16]), wk + ["off4_0"], ["Y%d%s" % (i, eng)], n, 256.0)
+        c += 2 * n
+        dma("s", T.y[:, c - 2 * n:c], T.Y[:, c - 2 * n:c], ["Y%dv" % i, "Y%da" % i], ["y%d" % i], "st", 0, 1500 + 1.3 * (P - c + 2 * n))
 
     Q = {"v": g.vector, "a": g.scalar, "p": g.tensor, "g": g, "s": g.sync}
     own = {"v": "sv", "a": "sa", "p": "sp", "g": "sq"}

@@ -10,10 +10,10 @@ OPT = {
     "raw": [3],
     "batches": [[0], [1, 2]],
     "multi": True, "passes": 3, "tol": 40.0,
-    "ring": 2, "scale": "aavvaavv", "l1": {"0": 1, "1": 4, "4": 4}, "dup": {"0": 2, "1": 2, "4": 1}, "hsplit": 1, "signs": [1, 2], "cuts": [[256], [256], [192, 64]],
-    "vg": [(0, 2, 0), (1, 2, 0), (1, 0, 0), (2, 2, 1)],
+    "ring": 2, "scale": "aaaaaaaa", "l1": {"0": 1, "1": 4, "4": 4}, "dup": {"0": 2, "1": 2, "4": 1}, "hsplit": 0, "signs": [1, 2, 4], "cuts": [[256], [256], [192, 64]],
+    "vg": [(0, 2, 0), (1, 2, 0), (2, 2, 0), (2, 2, 1)],
     "chunks": [256, 512, 640, 640],
-    "lat": 2500.0, "lats": 3000.0, "first": 1500.0, "load": 3000.0, "gap": 500.0, "wake": 80.0,
+    "lat": 1800.0, "lats": 3000.0, "first": 1500.0, "load": 3000.0, "gap": 500.0, "wake": 80.0,
 }
 
 SCRATCH = {"p" + b: ("psum", [128, 512], "float32") for b in "ABCDLMTF"}
@@ -21,7 +21,7 @@ for _dt, _bufs in (("bfloat16", dict(W=P + 12 * CAP, mt=128 * NMAT, iot=384, rst
                                      Ps=4 * 672, sg=18 * HW + 12 * 256, G=9 * CAP, out=12 * CAP)),
                    ("float16", dict(jh=FO + 256, i16=128)),
                    ("int32", dict(cm=384, fl=288, hh=32, pc=4, z=FO, u=FO, pp=FO, q=3 * CAP)),
-                   ("float32", dict(hf=32, C=32, i32=128, e8=128, o8=128, pf=16, tb=160, j0=256, jf=FO, m32=512, big=2 * (FO + 256), Y=P)),
+                   ("float32", dict(hf=32, C=32, i32=128, e8=128, o8=128, pf=16, tb=160, j0=256, jf=FO + 256, m32=640, big=2 * (FO + 256), Y=P)),
                    ("uint16", dict(Lo=192, Li=640, L3=144, off=FO + 256))):
     for _k in _bufs:
         SCRATCH[_k] = ("sbuf", [128, _bufs[_k]], _dt)
@@ -504,7 +504,11 @@ def rank_program(g, core, T, topo):
     for e in range(4):
         places(e)
         make(e)
-    ts(T.jh[:, FO:FO + 256], T.j0[:], col(T.pf, 3), None, A.subtract, None, ["j0", "pf"], ["jh4"], 256)
+    if 4 in OPT["signs"]:
+        act(col(T.pf, 4), col(T.pf, 3), AF.Identity, ["pf"], ["pf4"], 64, scale=-1.0, bias=0.5)
+        act(T.jf[:, FO:FO + 256], T.j0[:], AF.Identity, ["j0", "pf4"], ["jh4"], 256, bias=col(T.pf, 4))
+    else:
+        ts(T.jh[:, FO:FO + 256], T.j0[:], col(T.pf, 3), None, A.subtract, None, ["j0", "pf"], ["jh4"], 256)
     positions(4)
 
     win, wk = window(4)

from concourse.bass import DstId, RemoteDMATransfer
from concourse.mybir import AluOpType as A, ActivationFunctionType as AF

N, P, R, CAP = 4, 4096, 4, 256
HW = 144
FO = 4 * HW
ONES, TRI, E1, E2, B2, ID, ID4, IDN, FD, HALF, GD = 0, 1, 2, 6, 10, 11, 12, 13, 14, 17, 18
NMAT = 29
OPT = {
    "raw": [3],
    "batches": [[0], [1, 2]],
    "multi": True, "passes": 3, "tol": 40.0,
    "ring": 2, "scale": "aaaaaaaa", "l1": {"0": 1, "1": 4, "4": 4}, "dup": {"0": 2, "1": 2, "4": 1}, "hsplit": 0, "signs": [1, 2, 4], "cuts": [[256], [256], [192, 64]],
    "vg": [(0, 2, 0), (1, 2, 0), (2, 2, 0), (2, 2, 1)],
    "chunks": [256, 512, 640, 640],
    "lat": 1800.0, "lats": 3000.0, "first": 1500.0, "load": 3000.0, "gap": 500.0, "wake": 80.0,
}

SCRATCH = {"p" + b: ("psum", [128, 512], "float32") for b in "ABCDLMTF"}
for _dt, _bufs in (("bfloat16", dict(W=P + 12 * CAP, mt=128 * NMAT, iot=384, rst=288, crow=144, cb=288, F=672, S=672, Bb=1344, Rb=672,
                                     Ps=4 * 672, sg=18 * HW + 12 * 256, G=9 * CAP, out=12 * CAP)),
                   ("float16", dict(jh=FO + 256, i16=128)),
                   ("int32", dict(cm=384, fl=288, hh=32, pc=4, z=FO, u=FO, pp=FO, q=3 * CAP)),
                   ("float32", dict(hf=32, C=32, i32=128, e8=128, o8=128, pf=16, tb=160, j0=256, jf=FO + 256, m32=640, big=2 * (FO + 256), Y=P)),
                   ("uint16", dict(Lo=192, Li=640, L3=144, off=FO + 256))):
    for _k in _bufs:
        SCRATCH[_k] = ("sbuf", [128, _bufs[_k]], _dt)
SEMAPHORES = ["sv", "sa", "sp", "sq", "ld0", "ld1", "ld2", "ld3", "rg0", "rg1", "rg2", "rg3", "al0", "al1", "al2", "afl",
              "ar0", "ar1", "ar2", "ar3", "sent", "st", "stn"]

THR, MR, NG, WR, TH, SH, XU, ZU, CC, WE, KK, NW, H2, ZC, KS = 0, 16, 32, 48, 64, 80, 96, 112, 128, 132, 136, 140, 141, 142, 144


def dest_order(cores, q, topo):
    o = [(q - d) % N for d in range(1, N)]
    near = lambda r: topo.same_plane(topo.chip(cores[q]), topo.chip(cores[r]))
    return [r for r in o if not near(r)] + [r for r in o if near(r)]


def split_masks(engines):
    h, k = len(engines) // 2, len(engines) // 4
    parts = [engines[:h], engines[h:h + k], engines[h + k:h + 2 * k]]
    return [(sum(1 << e for e in p), len(p)) for p in parts]


def sweep(ops, before, after, lag, due, late):
    n = len(ops)
    left = [len(before[i]) for i in range(n)]
    start, free, todo = [None] * n, {}, {}
    for i in sorted(range(n), key=lambda i: (late[i], i)):
        todo.setdefault(ops[i]["e"], []).append(i)
        free[ops[i]["e"]] = 0.0
    pool = set(i for i in range(n) if not left[i])

    def soonest(i, t, memo):
        if i not in memo:
            memo[i] = max([due[i], t, free[ops[i]["e"]]] +
                          [soonest(j, t, memo) + ops[j]["c"] + lag(j, i) for j in before[i] if start[j] is None])
        return memo[i]

    shift = 0.0
    while pool:
        t, e = min((max(due[i], free[ops[i]["e"]]), ops[i]["e"]) for i in pool)
        memo, pick, ahead = {}, None, []
        for i in todo[e][:40]:
            if i in pool and due[i] <= t + 1e-6 and all(t + ops[i]["c"] <= max(s, late[m] + shift) + OPT["tol"] for m, s in ahead):
                pick = i
                break
            ahead.append((i, soonest(i, t, memo)))
        if pick is None:
            free[e] = min([s for m, s in ahead if s > t + 1e-6] or [t + 20.0])
            continue
        start[pick] = t
        shift = max(shift, t - late[pick])
        todo[e].remove(pick)
        pool.remove(pick)
        if e != "x":
            free[e] = t + ops[pick]["c"]
        for j in after[pick]:
            due[j] = max(due[j], t + ops[pick]["c"] + lag(pick, j))
            left[j] -= 1
            if not left[j]:
                pool.add(j)
    return start


def arrange(ops):
    n = len(ops)
    wr, rd = {}, {}
    for i, o in enumerate(ops):
        pre = set(wr[k] for k in o["r"] + o["w"] if k in wr)
        for k in o["w"]:
            pre.update(rd.get(k, []))
        for k in o["r"]:
            if k in SCRATCH and SCRATCH[k][0] == "psum":
                pre.update(j for j in rd.get(k, []) if ops[j]["e"] != o["e"])
        pre.discard(i)
        o["pre"] = sorted(pre)
        for k in o["r"]:
            rd.setdefault(k, []).append(i)
        for k in o["w"]:
            wr[k] = i
            rd[k] = []
    succ = [[] for _ in ops]
    for i, o in enumerate(ops):
        for j in o["pre"]:
            succ[j].append(i)
    lag = lambda i, j: 0.0 if ops[i]["e"] == ops[j]["e"] == "p" else ops[i]["l"]

    pre = [o["pre"] for o in ops]
    way = [0.0] * n
    for i in range(n - 1, -1, -1):
        way[i] = ops[i]["c"] + max([lag(i, j) + way[j] for j in succ[i]] or [ops[i]["l"]])
    late = [max(way) - w for w in way]
    best = None
    for _ in range(OPT["passes"] + 1):
        start = sweep(ops, pre, succ, lag, [0.0] * n, late)
        span = max(start[i] + ops[i]["c"] + ops[i]["l"] for i in range(n))
        if best is None or span < best[0]:
            best = (span, start)
        back = sweep(ops, succ, pre, lambda i, j: lag(j, i), [0.0 if succ[i] else ops[i]["l"] for i in range(n)],
                     [span - start[i] - ops[i]["c"] for i in range(n)])
        top = max(back[i] + ops[i]["c"] for i in range(n))
        late = [top - back[i] - ops[i]["c"] for i in range(n)]
    return sorted(range(n), key=lambda i: (best[1][i], i))


def rank_program(g, core, T, topo):
    rank = T.rank_of(core)
    if rank is None:
        return
    cores = list(T.cores)
    sem, tb = T.sem, T.tb
    ops = []

    def op(e, fn, r, w, c, l=OPT["wake"], tok=None):
        ops.append({"e": e, "fn": fn, "r": list(r), "w": list(w), "c": c, "l": l, "tok": tok})

    def cyc(n):
        return max(64, n) * 1.04

    def mms(bank, items):
        for i, (o, l, r_, reads, n) in enumerate(items):
            op("p", lambda o=o, l=l, r_=r_, a=i == 0, b=i == len(items) - 1: g.tensor.matmul(o, l, r_, a, b), reads, [bank], 20 + max(64, n) * 0.52)

    def ts(out, in0, s1, s2, o0, o1, r, w, n=64):
        if o1 is None:
            op("v", lambda: g.vector.tensor_scalar(out, in0, s1, None, o0), r, w, cyc(n))
        else:
            op("v", lambda: g.vector.tensor_scalar(out, in0, s1, s2, o0, o1), r, w, cyc(n))

    def tt(out, a, b, o, r, w, n=64):
        op("v", lambda: g.vector.tensor_tensor(out, a, b, o), r, w, cyc(n))

    def cp(out, a, r, w, n=64):
        op("v", lambda: g.vector.tensor_copy(out, a), r, w, cyc(n))

    def scan(out, a, b, init, r, w, n=64):
        op("v", lambda: g.vector.tensor_tensor_scan(out, a, b, init, A.mult, A.add), r, w, cyc(n))

    def fill(out, v, w, n=64):
        op("v", lambda: g.vector.memset(out, v), [], w, cyc(n))

    def act(out, a, f, r, w, n=128, **kw):
        op("a", lambda: g.scalar.activation(out, a, f, **kw), r, w, cyc(n) + 60)

    def iota(out, pat, base, cmul, key, n, **kw):
        op("g", lambda: g.iota(out, pat, base, cmul, **kw), [], [key], 160 + 2.1 * n)

    def dma(e, out, src, r, w, name, val, l):
        q = g.sync if e == "s" else g.scalar
        op(e, lambda: q.dma_start(out, src).then_inc(sem[name], 16), r, w, 60.0, l, (name, val))

    def mat(i):
        return T.mt[:, 128 * i:128 * (i + 1)]

    def mk(i):
        return "m%d" % i

    def col(buf, c):
        return buf[:, c:c + 1]

    raw = OPT["raw"]
    r0 = raw[0] if raw else 4
    dma("s", T.cm[:, 0:96], T.came[:, 0:96], [], ["cm0"], "ld0", 16, 2000.0)
    if raw:
        dma("s", T.cm[:, 96 * r0:96 * (raw[-1] + 1)], T.came[:, 96 * r0:96 * (raw[-1] + 1)], [], ["cm%d" % e for e in raw], "ld3", 16, 2200.0)
    rest = [e for e in range(1, 4) if e not in raw]
    dma("s", T.cm[:, 96 * rest[0]:96 * (rest[-1] + 1)], T.came[:, 96 * rest[0]:96 * (rest[-1] + 1)], [], ["cm%d" % e for e in rest], "ld1", 16, 2600.0)
    dma("a", T.hh[0:8, 0:27], T.hc[:], [], ["hh0"], "ld2", 32, 2100.0)
    dma("a", T.hh[0:8, 27:28], T.had[:], [], ["hh1"], "ld2", 32, 2100.0)
    nr = OPT["ring"]
    rw = P // nr
    for k in range(nr):
        dma("s", T.W[:, rw * k:rw * (k + 1)], T.ring[:, rw * k:rw * (k + 1)], [], ["W%d" % k], "rg%d" % k, 16,
            2600.0 + OPT["load"] * (k + 1) / nr)
    nload = len(ops)

    small = {"allow_small_or_imprecise_dtypes": True}
    iota(T.pc[:, 0:1], [[0, 1]], 0, 1, "pc0", 1)
    iota(T.iot[:, 0:128], [[1, 128]], 0, 0, "io0", 128, **small)
    iota(T.iot[:, 128:256], [[16, 8], [0, 16]], 0, 0, "io3", 128, **small)
    iota(T.iot[:, 256:384], [[16, 8], [0, 4], [1, 4]], 0, 0, "io2", 128, **small)
    fill(T.rst[:], 1.0, ["rst"], 144)
    fill(T.rst[:, 0:288:32], 0.0, ["rst"])
    fill(T.cb[:], 512.0, ["cb"], 144)
    fill(T.o8[0:8, :], 1.0, ["o8"], 128)
    for c, m in ((1, 124), (2, 115), (3, 112)):
        ts(col(T.pc, c), col(T.pc, 0), m, None, A.bitwise_and, None, ["pc0"], ["pc%d" % c])
    cp(T.pf[:, 0:4], T.pc[:, 0:4], ["pc0", "pc1", "pc2", "pc3"], ["pf"])
    io0 = T.iot[:, 0:128]
    ts(mat(ONES), T.iot[:, 128:256], col(T.pf, 3), None, A.is_equal, None, ["io3", "pf"], [mk(ONES)])
    ts(mat(ID), io0, col(T.pf, 0), None, A.is_equal, None, ["io0", "pf"], [mk(ID)])
    ts(T.i16[:], io0, col(T.pf, 0), None, A.is_equal, None, ["io0", "pf"], ["i16"])
    ts(mat(TRI), io0, col(T.pf, 0), -1.0, A.is_lt, A.mult, ["io0", "pf"], [mk(TRI)])
    tt(mat(TRI), mat(TRI), mat(ONES), A.mult, [mk(TRI), mk(ONES)], [mk(TRI)], 256)
    for a in range(4):
        ts(mat(E1 + a), io0, col(T.pf, 1), float(a), A.subtract, A.is_equal, ["io0", "pf"], [mk(E1 + a)])
        ts(mat(E2 + a), io0, col(T.pf, 2), float(4 * a), A.subtract, A.is_equal, ["io0", "pf"], [mk(E2 + a)])
    ts(mat(B2), T.iot[:, 256:384], col(T.pf, 2), 0.25, A.is_equal, A.mult, ["io2", "pf"], [mk(B2)])
    nbm = 3 * max(len(b) for b in OPT["batches"] + [raw])
    iota(T.crow[:, 0:16 * nbm], [[512, 4], [0, 4 * nbm]], 512, 0, "crow", 16 * nbm, **small)
    op("g", lambda: g.affine_select(T.e8[0:8, :], T.o8[0:8, :], [[1, 8], [0, 16]], A.is_equal, 0.0, 0, -1), ["o8"], ["e8"], 480.0)
    for i, sc in ((ID4, 0.25), (IDN, -1.0)):
        act(mat(i), mat(ID), AF.Copy, [mk(ID)], [mk(i)], scale=sc)
    act(T.i32[:], mat(ID), AF.Copy, [mk(ID)], ["i32"])

    def flags(src, lo, n, r, key):
        cp(T.F[:, lo:lo + n], src, r, ["F" + key], n)
        scan(T.S[:, lo:lo + n], T.rst[:, 0:n], T.F[:, lo:lo + n], 0.0, ["rst", "F" + key], ["S" + key], n // 2)

    def lists(lo, nb, key, b0, b1, b2):
        n = 32 * nb
        bl, dup = 2 * lo, OPT["dup"][key]
        Bb, Rb = T.Bb[:, bl:bl + n], T.Rb[:, lo:lo + n]
        pl = 4 * lo
        kb, kr = "Bb" + key, "Rb" + key
        kp = ["Ps%s_%d" % (key, a) for a in range(4)]
        ps = lambda a: T.Ps[:, pl + a * n:pl + (a + 1) * n]
        X = lambda b: T[b][:, 0:n]

        def split(bank, h):
            m = 1.5 * 2 ** 23 * 4 * h
            ts(Bb, X(bank), m, m, A.add, A.subtract, [bank], [kb], n)
            if h == 16 and dup == 2:
                ts(T.Bb[:, bl + n:bl + 2 * n], X(bank), m, m, A.add, A.subtract, [bank], [kb + "'"], n)
            tt(Rb, X(bank), Bb, A.subtract, [bank, kb], [kr], n)
            h = float(h)
            act(ps(1), Rb, AF.Relu, [kr], [kp[1]], n, bias=-h)
            for a, s1, s2, o0, o1 in ((0, 0.0, h, A.max, A.min), (2, h, 0.0, A.add, A.min), (3, -h, 0.0, A.max, A.min)):
                ts(ps(a), Rb, s1, s2, o0, o1, [kr], [kp[a]], n // 2)

        l1 = OPT["l1"][key]
        if l1 == 4:
            b2 = b0
        for b in sorted({b0, b2}):
            mms(b, [(X(b), mat(TRI), T.F[:, lo:lo + n], ["F" + key, mk(TRI)], n),
                    (X(b), mat(ONES), T.S[:, lo:lo + n], ["S" + key, mk(ONES)], n)])
        for a in range(4):
            if a < 4 - l1:
                ts(ps(a), X(b0), 0.25, 128 + (1.5 - a) / 4, A.mult, A.add, [b0], [kp[a]], n)
            else:
                act(ps(a), X(b2), AF.Identity, [b2], [kp[a]], n, scale=0.25, bias=128 + (1.5 - a) / 4)
        mms(b1, [(X(b1), mat(E1 + a), ps(a), [kp[a], mk(E1 + a)], n) for a in (0, 2, 1, 3)])
        split(b1, 4)
        mms(b0, [(X(b0), mat(B2), Bb, [kb, mk(B2)], n)] + [(X(b0), mat(E2 + a), ps(a), [kp[a], mk(E2 + a)], n) for a in (0, 2, 1, 3)])
        split(b0, 16)
        k = n // 4
        mms(b1, [(X(b1), mat(IDN), T.cb[:, 0:n], ["cb", mk(IDN)], n)] +
            [(T[b1][:, a * k:(a + dup) * k], mat(ID4), T.Bb[:, bl + c:bl + dup * n:4], [kb, kb + "'", mk(ID4)], dup * k)
             for a in range(0, 4, dup) for c in range(4)] +
            [(X(b1), mat(ID), T.Ps[:, pl + c:pl + 4 * n:4], kp + [mk(ID)], n) for c in range(4)])
        if nb > 3:
            act(Rb, X(b1), AF.Copy, [b1], [kr], n)
        for a in range(4):
            if nb > 3:
                ts(ps(a), Rb, 64.0 * a, 64.0 * a + 64.0, A.max, A.min, [kr], [kp[a]], n // 2)
            else:
                ts(ps(a), X(b1), 64.0 * a, 64.0 * a + 64.0, A.max, A.min, [b1], [kp[a]], n)
        w = 16 * nb
        mms(b0, [(T[b0][:, 0:w], mat(ID), T.crow[:, 0:16 * nbm:nbm // nb], ["crow", mk(ID)], w)] +
            [(T[b0][:, 0:w], mat(IDN), T.Ps[:, pl + c:pl + 4 * n:8], kp + [mk(IDN)], w) for c in range(8)])

    sent = [0]
    order = dest_order(cores, rank, topo)
    engines = topo.engines(core, cores[(rank + 1) % N])
    masks = split_masks(engines)
    nmask = sum(m[1] for m in masks)
    peer = lambda d: DstId(rid=topo.addr(cores[(rank + d) % N])[0], pnc=topo.addr(cores[(rank + d) % N])[1])

    def send(trs, name, r, w, after, n_out, n_in):
        op("g", lambda: g.remote_dma_fused(trs, local_sem=sem.sent), r, ["x" + name, "gl"], 300.0, 0.0, ("", 0))
        sent[0] += n_out
        op("x", None, ["x" + name], w, 0.0, after, (name, n_in))

    def to_makers(src, dst, name, r, w, after):
        send([RemoteDMATransfer(dst_ids=[peer(d)], dma_engine_mask=masks[d - 1][0], remote_sem=sem[name], src=src(d - 1), dst=dst(3 - d))
              for d in range(1, N)], name, r, w, after, nmask, nmask)

    xs = {}
    banks = [("pL", "pM", "pD"), ("pT", "pF", "pC"), ("pL", "pM", "pC")]
    first = OPT["first"]
    if raw:
        for e in raw:
            to_makers(lambda d: T.cm[:, 96 * e + 32 * d:96 * e + 32 * d + 32], lambda p: T.fl[:, 96 * (e - r0) + 32 * p:96 * (e - r0) + 32 * p + 32],
                      "afl", ["cm%d" % e], ["fl"], OPT["lats"] + first)
        ops[-1]["tok"] = ("afl", nmask * len(raw))
        first = 0.0
    for rounds in OPT["batches"]:
        e0, ne = rounds[0], len(rounds)
        flags(T.cm[:, 96 * e0:96 * (e0 + ne)], 96 * e0, 96 * ne, ["cm%d" % e for e in rounds], str(e0))

    def batch(i, first):
        rounds = OPT["batches"][i]
        e0, ne = rounds[0], len(rounds)
        key = str(e0)
        lo_i = 152 * e0
        lists(96 * e0, 3 * ne, key, *banks[i])
        k, o, b = 16 * ne, 48 * e0, banks[i][0]
        if OPT["multi"]:
            ts(T.Lo[:, o:o + 3 * k], T[b][:, 0:3 * k], 512.0 * rank, None, A.add, None, [b], ["Lo" + key], 3 * k)
            tr = RemoteDMATransfer(dst_ids=[peer(d) for d in range(1, N)], dma_engine_mask=sum(1 << e for e in engines), remote_sem=sem["al%d" % i],
                                   srcs=[T.Lo[:, o:o + 3 * k]],
                                   dsts=[T.Li[:, lo_i + (3 - d) * (3 * k + 1):lo_i + (3 - d) * (3 * k + 1) + 3 * k] for d in range(1, N)])
            send([tr], "al%d" % i, ["Lo" + key], ["Li" + key], OPT["lats"] + first, len(engines), 3 * len(engines))
            for e in rounds:
                xs[e] = (T.Li[:, lo_i + 2 + 3 * (e - e0):lo_i + 9 * k + 2:3 * ne], ["Li" + key])
        else:
            for d in range(3):
                ts(T.Lo[:, o + d * k:o + (d + 1) * k], T[b][:, d:3 * k:3], 512.0 * rank, None, A.add, None, [b], ["Lo%s_%d" % (key, d)])
            to_makers(lambda d: T.Lo[:, o + d * k:o + (d + 1) * k], lambda p: T.Li[:, o + p * k:o + (p + 1) * k],
                      "al%d" % i, ["Lo%s_%d" % (key, d) for d in range(3)], ["Li" + key], OPT["lats"] + first)
            for e in rounds:
                xs[e] = (T.Li[:, o + e - e0:o + 3 * k:ne], ["Li" + key])

    op("g", lambda: g.iota(T.j0[:], [[16, 256]], -2047, 1, **small), ["gl"], ["j0"], 700.0)
    batch(0, first)
    skeys = ["S%d" % b[0] for b in OPT["batches"]]
    if raw:
        flags(T.cm[:, 96 * r0:96 * (raw[-1] + 1)], 96 * r0, 96 * len(raw), ["cm%d" % e for e in raw], "r")
        skeys.append("Sr")
    mms("pB", [(T.pB[:, 0:12], mat(ONES), T.S[:, 31:384:32], skeys + [mk(ONES)], 64)])

    for k, eng in enumerate(OPT["scale"]):
        sl, key = T.W[:, 512 * k:512 * (k + 1)], "W%d" % (k * nr // 8)
        if eng == "a":
            act(sl, sl, AF.Copy, [key], ["V%d" % k], 512, scale=1.0 / 256)
        else:
            ts(sl, sl, 1.0 / 256, None, A.mult, None, [key], ["V%d" % k], 256)

    ts(T.hh[0:8, 28:29], T.hh[0:8, 27:28], 4095, None, A.bitwise_and, None, ["hh0", "hh1"], ["hh2"])
    cp(T.hf[0:8, 0:29], T.hh[0:8, 0:29], ["hh0", "hh1", "hh2"], ["hf"])
    mms("pA", [(T.pA[:, 0:29], T.e8[0:8, :], T.hf[0:8, 0:29], ["e8", "hf"], 256)])
    act(T.C[:, 0:29], T.pA[:, 0:29], AF.Copy, ["pA"], ["C"], 64)
    for k in range(3):
        act(mat(FD + k), mat(ID), AF.Copy, [mk(ID), "C"], [mk(FD + k)], scale=col(T.C, 24 + k))
    had, h0 = col(T.C, 27), col(T.C, 28)
    t12 = lambda c: tb[:, c:c + 12]
    t4 = lambda c: tb[:, c:c + 4]
    cnts, one = T.pB[:, 0:12], T.rst[:, 1:13]
    ts(col(tb, CC), had, 4096.0, 1.0 / 4096, A.min, A.mult, ["C"], ["cc0"])
    act(col(tb, H2), h0, AF.Identity, ["C"], ["h2"], 64, bias=-2047.0)
    act(col(tb, NW), h0, AF.Identity, ["C"], ["nw"], 64, bias=-4096.0)
    scan(t12(THR), one, cnts, col(tb, H2), ["rst", "pB", "h2"], ["thr"])
    scan(t12(MR), one, cnts, had, ["rst", "pB", "C"], ["mr"])
    ts(t12(NG), cnts, -256.0, None, A.add, None, ["pB"], ["ng"])
    for i in range(1, len(OPT["batches"])):
        batch(i, 0.0)
    ts(tb[:, CC + 1:CC + 4], tb[:, MR + 2:MR + 9:3], 4096.0, 1.0 / 4096, A.min, A.mult, ["mr"], ["cc1"])
    dma("s", T.now[:], tb[0:128:16, MR + 11:MR + 12], ["mr"], ["now"], "stn", 16, 2000.0)
    ts(t12(WR), t12(THR), 4096.0 - 2047.0, 4096.0, A.is_ge, A.mult, ["thr"], ["wr"])
    tt(t12(TH), t12(THR), t12(WR), A.subtract, ["thr", "wr"], ["th"])
    scan(t12(SH), one, t12(NG), col(tb, NW), ["rst", "ng", "nw"], ["sh"])
    tt(t4(WE), tb[:, WR + 2:WR + 12:3], tb[:, SH + 1:SH + 12:3], A.subtract, ["wr", "sh"], ["we"])
    tt(t12(XU), t12(NG), t12(WR), A.add, ["ng", "wr"], ["xu"])
    ts(t12(XU), t12(XU), 0.0, None, A.min, None, ["xu"], ["xu"])
    scan(t12(ZU), one, t12(XU), col(tb, NW), ["rst", "xu", "nw"], ["zu"])
    ts(t4(KK), tb[:, WR + 2:WR + 12:3], col(tb, ZU + 11), -1.0 / 4096, A.mult, A.mult, ["wr", "zu"], ["kk"])
    if OPT["signs"]:
        act(mat(HALF), mat(ID), AF.Copy, [mk(ID)], [mk(HALF)], scale=0.5)
        act(col(tb, ZC), col(tb, ZU + 11), AF.Identity, ["zu"], ["zc"], 64, scale=-1.0 / 4096, bias=0.5)
        act(t4(KS), tb[:, WR + 2:WR + 12:3], AF.Copy, ["wr", "zc"], ["ks"], 64, scale=col(tb, ZC))
        act(T.m32[:, 0:128], mat(HALF), AF.Copy, [mk(HALF), "nw"], ["w0"], scale=col(tb, NW))
        for e in OPT["signs"]:
            act(T.m32[:, 128 * e:128 * (e + 1)], mat(HALF), AF.Copy, [mk(HALF), "we"], ["w%d" % e], scale=col(tb, WE + e - 1))
        for b in range(3 * max(OPT["signs"]) - 1):
            act(mat(GD + b), mat(HALF), AF.Copy, [mk(HALF), "ng"], [mk(GD + b)], scale=col(tb, NG + b))

    if raw:
        ne = len(raw)
        flags(T.fl[:, 0:96 * ne], 384, 96 * ne, ["fl"], "4")
        lists(384, 3 * ne, "4", *banks[2])
        k = 16 * ne
        for p in range(3):
            ts(T.L3[:, k * p:k * p + k], T.pL[:, p:3 * k:3], 512.0 * ((rank - 3 + p) % N), None, A.add, None, ["pL"], ["L3_%d" % p])
        for e in raw:
            xs[e] = (T.L3[:, e - r0:3 * k:ne], ["L3_0", "L3_1", "L3_2"])

    def places(e):
        x, xk = xs[e]
        for ks in ([[2], [0], [1]] if e < OPT["hsplit"] else [[0, 1, 2]]):
            o, n = e * HW + 48 * ks[0], 48 * len(ks)
            name = lambda s: ["%s%d_%d" % (s, e, k) for k in ks]
            z, u, s, pp = T.z[:, o:o + n], T.u[:, o:o + n], T.pD[:, 0:n], T.pp[:, o:o + n]
            for k in ks:
                c = e * HW + 48 * k
                ts(T.z[:, c:c + 48], x, col(T.C, 6 * e + k), col(T.C, 6 * e + 3 + k), A.mult, A.add, xk + ["C"], ["z%d_%d" % (e, k)])
            ts(u, z, 4095, None, A.bitwise_and, None, name("z"), name("u"), n)
            if len(ks) == 1:
                ts(pp, u, 2.0, -4095.0, A.mult, A.add, name("u"), name("pp"), n)
                tt(z, u, pp, A.mult, name("u") + name("pp"), name("z"), 2 * n)
            else:
                ts(s, u, 2.0, -4095.0, A.mult, A.add, name("u"), ["pD"], n)
                tt(z, u, s, A.mult, name("u") + ["pD"], name("z"), n)
            ts(u, z, 4095, None, A.bitwise_and, None, name("z"), name("u"), n)
            ts(pp, u, col(tb, CC + e), -2047.5 + 2.0 ** -13, A.mult, A.add, name("u") + ["cc1" if e else "cc0"], name("pp"), n)
            if e == 0:
                ts(T.off[:, o:o + n], pp, 2047.0, None, A.add, None, name("pp"), name("off"), n)
            elif e in OPT["signs"]:
                ts(T.jf[:, o:o + n], pp, 0.5, None, A.add, None, name("pp"), ["jh%d" % e], n)
            else:
                cp(T.jh[:, o:o + n], pp, name("pp"), ["jh%d" % e], n)
        if e:
            positions(e)

    def positions(e):
        o, n, bank = (e * HW, HW, "pL" if e in raw else "pT") if e < 4 else (FO, 256, "pF")
        jh, kj = T.jh[:, o:o + n], "jh%d" % e
        so = HW * (3 * e * (e - 1) // 2)
        X = T[bank][:, 0:n]
        if e in OPT["signs"]:
            jf = T.jf[:, o:o + n]
            items = [(X, T.i32[:], jf, ["i32", kj], 4 * n)]
            for b in [0, 3 * e] + list(range(1, 3 * e)):
                k, c = "sg%d_%d" % (e, b), o + (FO + 256) * (b > 0)
                sl = T.big[:, c:c + n] if b in (0, 3 * e) else T.sg[:, so + b * n:so + (b + 1) * n]
                act(sl, jf, AF.Sign, [kj, "th", "h2"], [k], n, bias=col(tb, TH + b - 1) if b else col(tb, H2), scale=-1.0)
                if b in (0, 3 * e):
                    i = e if b else 0
                    items.append((X, T.m32[:, 128 * i:128 * (i + 1)], sl, [k, "w%d" % i], 4 * n))
                else:
                    items.append((X, mat(GD + b - 1), sl, [k, mk(GD + b - 1)], n))
            mms(bank, items)
            ts(T.off[:, o:o + n], X, col(tb, KS + e - 1), 2046.5, A.add, A.add, [bank, "ks"], ["off%d_%d" % (e, k) for k in range(3)], n)
            return
        items = [(X, T.i16[:], jh, ["i16", kj], n)]
        for b in [0, 3 * e] + list(range(1, 3 * e)):
            k = "sg%d_%d" % (e, b)
            th = col(tb, TH + b - 1) if b else col(tb, H2)
            if b in (0, 3 * e):
                c = o + (FO + 256) * (b > 0)
                ts(T.big[:, c:c + n], jh, th, col(tb, WE + e - 1) if b else col(tb, NW), A.is_lt, A.mult, [kj, "th", "h2", "nw", "we"], [k], n)
                items.append((X, T.i32[:], T.big[:, c:c + n], [k, "i32"], 4 * n))
            else:
                sl = T.sg[:, so + b * n:so + (b + 1) * n]
                ts(sl, jh, th, col(tb, NG + b - 1), A.is_lt, A.mult, [kj, "th", "ng"], [k], n // 2)
                items.append((X, mat(ID), sl, [k, mk(ID)], n))
        mms(bank, items)
        ts(T.off[:, o:o + n], X, col(tb, KK + e - 1), 2047.0, A.add, A.add, [bank, "kk"], ["off%d_%d" % (e, k) for k in range(3)], n)

    def window(e):
        return T.W[:, 0:P + 3 * CAP * e], ["V%d" % k for k in range(8)] + ["land%d_%d" % (i, j) for i in range(e) for j in range(3)]

    def gather(eng, dst, src, r, w, n, scale=None):
        c = (1.56 * n + 50) * 1.04
        if eng == "a":
            op("a", lambda: g.scalar.activation(dst, src, AF.Copy, scale=scale or 1.0), r, w, c + 15)
        elif scale:
            op("v", lambda: g.vector.tensor_scalar(dst, src, scale, None, A.mult), r, w, c)
        else:
            op("v", lambda: g.vector.tensor_copy(dst, src), r, w, c)

    def make(e):
        win, wk = window(e)
        for j in range(3):
            r = order[j]
            piece = 3 - (rank - r) % N
            oo, a, done = (3 * e + j) * CAP, 0, []
            for i, n in enumerate(OPT["cuts"][j]):
                bank = ("pA", "pB", "pC")[j] if i == 0 else "pA"
                x, qq = T[bank][:, 0:n], T.q[:, j * CAP + a:j * CAP + a + n]
                items = []
                for k in (2, 0, 1):
                    c = e * HW + 48 * k + 16 * piece + a // 16
                    go, key = (3 * j + k) * CAP + a, "G%d_%d_%d" % (j, k, i)
                    gather("v" if (j, k, i) in OPT["vg"] else "a", T.G[:, go:go + n], win.indirect(T.off[:, c:c + n // 16]),
                           wk + ["off%d_%d" % (e, k)], [key], n)
                    items.append((x, mat(FD + k), T.G[:, go:go + n], [key, mk(FD + k)], n))
                mms(bank, items)
                done.append("o%d_%d" % (3 * e + j, i))
                ts(qq, x, -127.5 / 256, None, A.add, None, [bank], ["q%d_%d" % (j, i)], n)
                tt(T.out[:, oo + a:oo + a + n], x, qq, A.subtract, [bank, "q%d_%d" % (j, i)], done[-1:], n)
                a += n
            o = T.out[:, oo:oo + CAP]
            rid, pid, _ = topo.addr(cores[r])
            c = P + (3 * e + (rank - r) % N - 1) * CAP
            op("g", lambda c=c, o=o, r=r, pid=pid, rid=rid: g.remote_dma(T.W[:, c:c + CAP], o, sem["ar%d" % e], sem.sent, pid, rid,
                                                                         topo.mask(core, cores[r])),
               done, ["x%d_%d" % (e, j), "gq"], 300.0, 0.0, ("", 0))
            sent[0] += len(topo.engines(core, cores[r]))
            op("x", None, ["x%d_%d" % (e, j)], ["land%d_%d" % (e, j)], 0.0, OPT["lat"] + OPT["gap"] * (2 - j),
               ("ar%d" % e, sum(len(topo.engines(cores[q], core)) for q in range(N) if q != rank)))

    for e in range(4):
        places(e)
        make(e)
    if 4 in OPT["signs"]:
        act(col(T.pf, 4), col(T.pf, 3), AF.Identity, ["pf"], ["pf4"], 64, scale=-1.0, bias=0.5)
        act(T.jf[:, FO:FO + 256], T.j0[:], AF.Identity, ["j0", "pf4"], ["jh4"], 256, bias=col(T.pf, 4))
    else:
        ts(T.jh[:, FO:FO + 256], T.j0[:], col(T.pf, 3), None, A.subtract, None, ["j0", "pf"], ["jh4"], 256)
    positions(4)

    win, wk = window(4)
    c = 0
    for i, n in enumerate(OPT["chunks"]):
        for h, eng in enumerate("va"):
            a = c + h * n
            gather(eng, T.Y[:, a:a + n], win.indirect(T.off[:, FO + a // 16:FO + (a + n) // 16]), wk + ["off4_0"], ["Y%d%s" % (i, eng)], n, 256.0)
        c += 2 * n
        dma("s", T.y[:, c - 2 * n:c], T.Y[:, c - 2 * n:c], ["Y%dv" % i, "Y%da" % i], ["y%d" % i], "st", 0, 1500 + 1.3 * (P - c + 2 * n))

    Q = {"v": g.vector, "a": g.scalar, "p": g.tensor, "g": g, "s": g.sync}
    own = {"v": "sv", "a": "sa", "p": "sp", "g": "sq"}
    cnt = {"sv": 0, "sa": 0, "sp": 0, "sq": 0}
    waited = {k: {} for k in Q}

    def wait(e, name, val):
        if name and waited[e].get(name, 0) < val:
            Q[e].wait_ge(sem[name], val)
            waited[e][name] = val

    for i in list(range(nload)) + [i for i in arrange(ops) if i >= nload]:
        o = ops[i]
        e = o["e"]
        if e == "x":
            continue
        need = {}
        for j in o["pre"]:
            name, val = ops[j]["tok"]
            if not (e == "p" and name == "sp"):
                need[name] = max(need.get(name, 0), val)
        for name in need:
            wait(e, name, need[name])
        ins = o["fn"]()
        if o["tok"] is None:
            cnt[own[e]] += 1
            ins.then_inc(sem[own[e]], 1)
            o["tok"] = (own[e], cnt[own[e]])
    for name in cnt:
        wait("g", name, cnt[name])
    wait("g", "sent", sent[0])
    wait("s", "stn", 16)
    wait("s", "st", 16 * len(OPT["chunks"]))
